import numpy as np, ml_dtypes
CORES = [35,38,43,46]
N = 4
BF = ml_dtypes.bfloat16
def f(rng, *shape):
    return (rng.standard_normal(shape, dtype=np.float32) * np.exp2(rng.integers(-2, 3, shape[:-1] + (1,)))).astype(BF)
def wide(rng, *shape):
    v = f(rng, *shape).astype(np.float32); k = shape[:-2] + (1, shape[-1])
    return (v * np.exp2(rng.integers(-6, 7, k)) * (rng.random(k) > 0.0625)).astype(BF)
def gentries(a):
    return np.ascontiguousarray(a.reshape(8, 16, -1).transpose(0, 2, 1)).reshape(8, -1)
def gtable(e):
    e = np.asarray(e); return np.ascontiguousarray(e.reshape(8, -1, 16).transpose(0, 2, 1)).reshape(128, -1).astype(np.int32)
NV, NC, E, B, CX, A, KN = 4096, 512, 4096, 256, 96, 256, 16
def lists8(a):
    return np.stack([gentries(v) for v in a])
def tables8(e):
    return np.stack([gtable(v) for v in e])
def cases(s, cor):
    t = np.take_along_axis(s, lists8(cor), -1).reshape(N, 8, 8, NC).astype(np.int64)
    return np.sum(t << np.arange(8)[:, None], axis=2)
def crossings(s, bl):
    w = np.take_along_axis(s, lists8(bl), -1).reshape(N, 8, N, B).transpose(0, 2, 1, 3)
    return w != w.transpose(1, 0, 2, 3)
def pick(rng, s, want, h):
    o = np.argsort(s, axis=-1, kind="stable"); n0 = NV - np.sum(s, axis=-1, keepdims=True)
    u = rng.integers(0, 4, want.shape) * 0.25 if h else rng.random(want.shape)
    i = np.where(want, n0 + np.minimum(np.floor(u * (NV - n0)), NV - n0 - 1), np.minimum(np.floor(u * n0), n0 - 1)).astype(np.int64)
    return np.take_along_axis(o, i, -1)
def make(rng, act, cross, zero=0.0625, h=False):
    s = rng.random((N, 8, NV)) < rng.uniform(0.3, 0.7, (N, 8, 1))
    m = (rng.random(s.shape) + 0.0625) * np.exp2(rng.integers(-3, 4, s.shape))
    z = np.where(rng.random(s.shape) < 0.5, 0.0, -0.0)
    lv = np.where(s, -m, np.where(rng.random(s.shape) < zero, z, m)).astype(BF)
    key = rng.random((N, 8, NC)); key[..., 0] -= rng.integers(0, 2, (N, 8)); key[..., -1] -= rng.integers(0, 2, (N, 8))
    on = (np.argsort(np.argsort(key, axis=-1), axis=-1) < act[..., None])[:, :, None]
    k = np.arange(8)[:, None]; c1 = rng.integers(0, 8, (N, 8, 1, NC)); c2 = (c1 + rng.integers(1, 8, c1.shape)) % 8
    w = (rng.random((N, 8, 8, NC)) < 0.5) & (k != c2) | (k == c1)
    w = np.where(on, w, rng.random((N, 8, 1, NC)) < 0.5)
    wa = rng.random((N, 8, E)) < 0.5; x = rng.random((N, 8, E)) < 0.75; x[..., 0] = True; x[..., -1] = True
    wb = wa ^ x
    c = np.argsort(rng.random((N, N, 8, B)), axis=-1) < cross[..., None]
    b = rng.random((N, N, 8, B)) < 0.5
    for q in range(N):
        for r in range(q + 1, N): b[r, q] = b[q, r] ^ c[q, r]
    tab = rng.integers(0, 12, (N, 16, 256 * KN)); tab[rng.random(tab.shape) < 0.2] = -1
    return {"lv": lv, "ch": f(rng, N, 128, NV), "cor": tables8(pick(rng, s, w.reshape(N, 8, 8 * NC), h)), "kd": rng.integers(0, KN, (N, 8, NC)).astype(np.int32),
            "ce": rng.integers(0, E + N * B, (N, 8, 12 * NC)).astype(np.int32), "ea": tables8(pick(rng, s, wa, h)), "eb": tables8(pick(rng, s, wb, h)),
            "bl": tables8(pick(rng, s, b.transpose(0, 2, 1, 3).reshape(N, 8, N * B), h)), "tab": tab.astype(np.int32)}
def sizes(rng):
    act = rng.integers(A >> 1, A + 1, (N, 8)); act[rng.integers(0, N), rng.integers(0, 8)] = A
    cross = rng.integers(CX >> 1, CX + 1, (N, N, 8)); q, r = np.sort(rng.choice(N, 2, replace=False)); cross[q, r, rng.integers(0, 8)] = CX
    return act, cross
def setup_inputs(rng):
    return make(rng, *sizes(rng))
def setup_inputs_full(rng):
    return make(rng, np.full((N, 8), A), np.full((N, N, 8), CX))
def setup_inputs_few(rng):
    act = rng.choice(np.array([0, 1, A >> 2]), (N, 8)); act[np.arange(N), rng.integers(0, 8, N)] = A >> 2
    return make(rng, act, rng.choice(np.array([0, 1, CX]), (N, N, 8)))
def setup_inputs_zeros(rng):
    d = make(rng, *sizes(rng), zero=0.5); tab = d["tab"]; w = rng.integers(0, 6, (N, 1, 256 * KN)); e = rng.integers(0, 12, w.shape).astype(np.int32)
    tab = np.where(w == 0, -1, np.where(w == 1, e, tab)); tab = np.where((w == 2) & (np.arange(16)[:, None] < 15), -1, np.where(w == 2, e, tab))
    d["tab"] = tab.astype(np.int32); return d
def setup_inputs_alike(rng):
    d = make(rng, *sizes(rng), h=True); p = rng.integers(0, E + N * B, (N, 8, 8)); p[..., 0] = 0; p[..., 1] = E + N * B - 1
    d["ce"] = np.take_along_axis(p, rng.integers(0, 8, (N, 8, 12 * NC)), -1).astype(np.int32)
    d["kd"] = np.repeat(rng.integers(0, KN, (N, 8, 1)), NC, axis=-1).astype(np.int32); return d
def setup_inputs_spread(rng):
    d = setup_inputs(rng); d["ch"] = wide(rng, N, 128, NV)
    d["lv"] = (d["lv"].astype(np.float32) * np.exp2(rng.integers(-6, 7, d["lv"].shape))).astype(BF); return d
def check_inputs(d):
    bad = [a for a, lo, hi in (("cor", 0, NV - 1), ("kd", 0, KN - 1), ("ce", 0, E + N * B - 1), ("ea", 0, NV - 1), ("eb", 0, NV - 1), ("bl", 0, NV - 1), ("tab", -1, 11)) if d[a].min() < lo or d[a].max() > hi]
    bad += [a for a in ("lv", "ch") if not np.isfinite(d[a].astype(np.float32)).all()]
    if bad: return bad
    s = d["lv"].astype(np.float32) < 0; c = cases(s, d["cor"])
    if np.sum((c > 0) & (c < 255), axis=-1).max() > A: bad.append("active cells")
    if np.sum(crossings(s, d["bl"]), axis=-1).max() > CX: bad.append("crossing border edges")
    return bad
def reference(lv, ch, cor, kd, ce, ea, eb, bl, tab):
    y = np.zeros((N, 128, 16 * A), np.float32); zero = np.float32(0)
    s = lv.astype(np.float32) < 0; c = ch.astype(np.float32).reshape(N, 8, 16, NV)
    case = cases(s, cor); cross = crossings(s, bl); la, lb, lx = lists8(ea), lists8(eb), lists8(bl).reshape(N, 8, N, B)
    for r in range(N):
        for g in range(8):
            v = np.zeros((16, E + N * B), np.float32); i, j = la[r, g], lb[r, g]
            v[:, :E] = np.where(s[r, g][i] != s[r, g][j], c[r, g][:, i] + c[r, g][:, j], zero)
            for q in range(N):
                v[:, E + q * B:E + (q + 1) * B] = np.where(cross[r, q, g], c[r, g][:, lx[r, g, q]] + c[q, g][:, lx[q, g, r]], zero)
            m = np.flatnonzero((case[r, g] > 0) & (case[r, g] < 255))
            e = tab[r][:, 256 * kd[r, g, m] + case[r, g, m]].T
            n = ce[r, g][12 * m[:, None] + np.maximum(e, 0)].reshape(-1)
            y[r, 16 * g:16 * g + 16, :16 * len(m)] = np.where(e.reshape(-1) >= 0, v[:, n], zero)
    return {"y": y}

@@ -1,0 +1,370 @@
+from concourse.bass import DstId, RemoteDMATransfer
+from concourse.mybir import AluOpType, ActivationFunctionType
+
+ALU = AluOpType
+ID = ActivationFunctionType.Identity
+RELU = ActivationFunctionType.Relu
+NV, NB, NA = 4096, 256, 256
+PAD = 16
+TOP = PAD + NV + 4 * NB
+BIG = 8192.0
+CUTS = [0, 512, 1024, 1792, 2560, 3328, 3840, 4096]
+CC = [0, 48, 96, 144, 192]
+XA = [16, 32, 20, 32]
+BANKS = [(6, 7), (0, 1), (2, 3), (6, 7)]
+YS = [(0, 28), (28, 64), (64, 96), (96, 120), (120, 142), (142, 192), (192, 222), (222, 240), (240, 256)]
+YQ = "VAAVAVAAV"
+ORDER = ("k0 x0 y0 x1 e0 e1 l0 x2 m0 a00 e2 x3 v00 e3 l1 a01 o0 v01 a10 m1 v10 a11 l2 o1 o2 a20 v11 m2 a21 o3 l3 v20 "
+         "o4 a30 v21 m3 o5 v30 a31 o6 v31 o7 o8").split()
+
+F, B, I, U, H = "float32", "bfloat16", "int32", "uint16", "float16"
+SCRATCH = {
+    "W": ("sbuf", [128, NV], B), "X": ("sbuf", [128, NV + 4 * NB], B), "CH": ("sbuf", [128, TOP + 16], B),
+    "TAB": ("sbuf", [128, 16 + NV], B), "tbi": ("sbuf", [128, 512], I), "tbb": ("sbuf", [128, 512], B),
+    "GA": ("sbuf", [128, 2048], B), "GV": ("sbuf", [128, 2048], B), "sb": ("sbuf", [128, 256], B),
+    "UE": ("sbuf", [128, NV], B), "XL": ("sbuf", [128, 3072], B), "CA": ("sbuf", [128, 3072], B),
+    "VC": ("sbuf", [128, PAD + 3072], F), "Y": ("sbuf", [128, 4096], F),
+    "MS": ("sbuf", [128, 4 * NB], B), "MC": ("sbuf", [128, 4 * NB], B),
+    "lvc": ("sbuf", [128, 256], B), "sc": ("sbuf", [128, 256], B),
+    "cori": ("sbuf", [128, 256], I), "eai": ("sbuf", [128, 256], I), "ebi": ("sbuf", [128, 256], I),
+    "bli": ("sbuf", [128, 64], I), "coru": ("sbuf", [128, 256], U), "eau": ("sbuf", [128, 256], U),
+    "ebu": ("sbuf", [128, 256], U), "blu": ("sbuf", [128, 64], U),
+    "kdi": ("sbuf", [128, 512], I), "kdb": ("sbuf", [128, 512], B),
+    "cei": ("sbuf", [128, 32, 12], I), "cep": ("sbuf", [128, 32, 16], F),
+    "pi": ("sbuf", [128, 48], I), "col": ("sbuf", [128, 64], F),
+    "jj": ("sbuf", [128, 64], F), "mk": ("sbuf", [128, 64], F), "oh": ("sbuf", [128, 16], F),
+    "ones": ("sbuf", [128, 144], F), "lb": ("sbuf", [128, 128], F), "lk": ("sbuf", [128, 1024], B),
+    "idf": ("sbuf", [128, 128], F), "idb": ("sbuf", [128, 128], B),
+    "z0": ("sbuf", [128, 144], F), "zq": ("sbuf", [128, 144], H), "za": ("sbuf", [128, 144], B),
+    "zv": ("sbuf", [128, 144], B), "zk": ("sbuf", [128, 144], B),
+    "kdl": ("sbuf", [128, 128], B), "pk": ("sbuf", [128, 6, 8, 16], F),
+    "dump": ("sbuf", [128, 32], F), "cm": ("sbuf", [128, 256], F), "keep": ("sbuf", [128, 512], B),
+    "ee": ("sbuf", [128, 512], H), "cum": ("sbuf", [128, 512], H),
+    "tf": ("sbuf", [128, 32], F), "tu": ("sbuf", [128, 32], U),
+    "cev": ("sbuf", [128, 512], F), "S": ("sbuf", [128, 896], F),
+    "cel": ("sbuf", [128, 192], U), "kcu": ("sbuf", [128, 16], U),
+    "tt": ("sbuf", [128, 256], B), "tn": ("sbuf", [128, 256], B), "yl": ("sbuf", [128, 256], U),
+    "al": ("sbuf", [128, 192], U), "vl": ("sbuf", [128, 192], U),
+}
+for _k in range(8):
+    SCRATCH["P%d" % _k] = ("psum", [128, 512], F)
+SEMAPHORES = ["sV", "sA", "sP", "sG", "arrS", "arrC", "sentS", "sentC"] + ["d%d" % k for k in range(30)]
+
+
+def engine_sets(topo, src, dsts):
+    sets, used = {}, set()
+    order = sorted(dsts, key=lambda d: len(topo.engines(src, d)))
+    for k, d in enumerate(order):
+        mine = topo.engines(src, d)
+        left = [e for e in mine if e not in used]
+        rivals = len([p for p in order[k:] if topo.engines(src, p) == mine])
+        n = 1
+        while 2 * n * rivals <= len(left):
+            n *= 2
+        used.update(left[:n])
+        sets[d] = left[:n]
+    return sets
+
+
+def rank_program(g, core, T, topo):
+    rank = T.rank_of(core)
+    if rank is None:
+        return
+    N = len(T.cores)
+    peers = [q for q in range(N) if q != rank]
+    Q = {"V": g.vector, "A": g.scalar, "P": g.tensor, "G": g, "S": g.sync}
+    cnt = {}
+    seen = {}
+    nd = [0]
+
+    def wait(q, deps):
+        need = {}
+        for d in deps:
+            if d is not None:
+                need[d[0]] = max(need.get(d[0], 0), d[1])
+        for s, n in need.items():
+            if seen.get((q, s), 0) < n:
+                Q[q].wait_ge(T.sem[s], n)
+                seen[(q, s)] = n
+
+    def op(q, deps, fn, mark=True):
+        wait(q, deps)
+        ins = fn(Q[q])
+        if not mark:
+            return None
+        s = "s" + q
+        cnt[s] = cnt.get(s, 0) + 1
+        ins.then_inc(T.sem[s], 1)
+        return (s, cnt[s])
+
+    def dma(q, deps, pairs):
+        wait(q, deps)
+        s = "d%d" % nd[0]
+        nd[0] += 1
+        for o, i in pairs:
+            Q[q].dma_start(o, i).then_inc(T.sem[s], 16)
+        cnt[s] = 16 * len(pairs)
+        return (s, cnt[s])
+
+    def ts(deps, o, i, s1, op0, s2=None, op1=None):
+        if op1 is None:
+            return op("V", deps, lambda e: e.tensor_scalar(o, i, s1, None, op0))
+        return op("V", deps, lambda e: e.tensor_scalar(o, i, s1, s2, op0, op1))
+
+    def cp(deps, o, i):
+        return op("V", deps, lambda e: e.tensor_copy(o, i))
+
+    def tt(deps, o, a, b, alu):
+        return op("V", deps, lambda e: e.tensor_tensor(o, a, b, alu))
+
+    def act(deps, o, i, scale=1.0, bias=0.0, func=ID):
+        return op("A", deps, lambda e: e.activation(o, i, func, bias=bias, scale=scale))
+
+    def mm(deps, o, l, r, start, stop, mark=True):
+        return op("P", deps, lambda e: e.matmul(o, l, r, start, stop), mark)
+
+    def sel(deps, o, i, pat, cmp, base, cm=1):
+        return op("G", deps, lambda e: e.affine_select(o, i, pat, cmp, 0.0, base, cm))
+
+    def iota(o, pat, base, cm, fl=True):
+        if fl:
+            return op("G", [], lambda e: e.iota(o, pat, base, cm, allow_small_or_imprecise_dtypes=True))
+        return op("G", [], lambda e: e.iota(o, pat, base, cm))
+
+    def extract(deps, o, z, src, lo, hi):
+        t = None
+        for u in range(16):
+            t = mm(deps, o, z[:, 15 - u:143 - u], src[:, lo + u:hi:16], u == 0, u == 15, mark=(u == 15))
+        return t
+
+    others = [T.cores[q] for q in peers]
+    eng = engine_sets(topo, core, others)
+    n_out = sum(len(v) for v in eng.values())
+    n_in = sum(len(engine_sets(topo, c, [d for d in T.cores if d != c])[core]) for c in others)
+
+    def send(deps, src, dst, lo_src, lo_dst, arr, sent):
+        wait("G", deps)
+        tr = []
+        for q in peers:
+            rid, pid, _ = topo.addr(T.cores[q])
+            a, b = lo_src + NB * q, lo_dst + NB * rank
+            tr.append(RemoteDMATransfer(dst_ids=[DstId(rid=rid, pnc=pid)],
+                                        dma_engine_mask=sum(1 << e for e in eng[T.cores[q]]),
+                                        remote_sem=T.sem[arr], src=src[:, a:a + NB], dst=dst[:, b:b + NB]))
+        g.remote_dma_fused(tr, local_sem=T.sem[sent])
+        cnt[sent], cnt[arr] = n_out, n_in
+        return (sent, n_out), (arr, n_in)
+
+    C = lambda k: T.col[:, k:k + 1]
+    OH = lambda j: T.oh[:, j:j + 1]
+    P = [T["P%d" % k] for k in range(8)]
+    blocks = [b for b in [(0, rank), (rank + 1, N)] if b[1] > b[0]]
+
+    l_lv = dma("S", [], [(T.lvc[:], T.lv[:])])
+    l_cor = dma("S", [], [(T.cori[:], T.cor[:])])
+    l_kd = dma("S", [], [(T.kdi[0:8, :], T.kd[:])])
+    l_ce = dma("S", [], [(T.cei[:, 4 * k:4 * k + 4, :], T.ce[k]) for k in range(8)])
+
+    g_p = iota(T.pi[:, 0:16], [[-1, 16]], 16, 1, False)
+    g_j = iota(T.jj[:], [[1, 64]], 0, 0)
+    g_cm = iota(T.cm[:], [[-12, 256]], -PAD, 0)
+    t = ts([g_p], T.pi[:, 16:18], T.pi[:, 0:2], 7, ALU.bitwise_and)
+    v_a = ts([g_p], T.pi[:, 32:48], T.pi[:, 0:16], 15, ALU.bitwise_and)
+    t = ts([t], T.col[:, 0:2], T.pi[:, 16:18], 0.0, ALU.is_equal)
+    ts([t, g_j], T.W[:, 0:64], T.jj[:], float(PAD), ALU.add, C(1), ALU.mult)
+    t = ts([t, g_j], T.mk[:], T.jj[:], 64.0, ALU.mult, C(0), ALU.mult)
+    for n in (64, 256):
+        for j in (1, 2, 3):
+            t2 = ts([t], T.W[:, n * j:n * j + n], T.W[:, 0:n], T.mk[:, n * j // 64:n * j // 64 + 1], ALU.add)
+        t = t2
+
+    def fill(o, n, val):
+        return act([g_cm], o, T.cm[:, 0:n], 0.0, val)
+
+    a_one = fill(T.ones[:], 144, 1.0)
+    a_cz = fill(T.cep[:, :, 12:16], 128, 0.0)
+    fill(T.X[:, NV + NB * rank:NV + NB * rank + NB], NB, -1.0)
+    a_w = act([t], T.W[:, 3072:4096], T.W[:, 0:1024], 1.0, T.mk[:, 48:49])
+    ts([t], T.W[:, 1024:2048], T.W[:, 0:1024], T.mk[:, 16:17], ALU.add)
+    ts([l_lv], T.sc[:], T.lvc[:], 0.0, ALU.is_lt, 0.5, ALU.subtract)
+    v_s = ts([t], T.W[:, 2048:3072], T.W[:, 0:1024], T.mk[:, 32:33], ALU.add)
+    w_s = dma("S", [a_w, v_s], [(T.W[2::16, :], T.sc[:])])
+    l_bl = dma("S", [], [(T.bli[:], T.bl[:])])
+    l_ea = dma("S", [], [(T.eai[:], T.ea[:])])
+    l_eb = dma("S", [], [(T.ebi[:], T.eb[:])])
+    l_tb = dma("S", [], [(T.tbi[:], T.tab[:])])
+    sl = PAD + NV + NB * rank
+    l_ch = dma("S", [], [(T.CH[:, PAD:PAD + NV], T.ch[:]), (T.CH[:, sl:sl + NB], T.ch[:, 0:NB])])
+    Wt = [w_s]
+
+    v_oh = ts([v_a], T.oh[:], T.pi[:, 32:48], 0.0, ALU.is_equal)
+    v_cor = cp([l_cor], T.coru[:], T.cori[:])
+    v_kd = ts([l_kd], T.kdb[0:8, :], T.kdi[0:8, :], 256.0, ALU.mult)
+    ts([v_a], C(2), T.pi[:, 32:33], 2.0, ALU.is_ge)
+    ts([v_a], C(5), T.pi[:, 32:33], 2.0, ALU.is_ge, 255.0, ALU.mult)
+    v_keep = ts([v_oh], C(13), OH(1), OH(2), ALU.add, OH(3), ALU.add)
+    for c in range(4):
+        v_ce = cp([l_ce, a_cz], T.cep[:, 8 * c:8 * c + 8, 0:12], T.cei[:, c::4, :])
+    ts([v_oh], C(6), OH(0), OH(4), ALU.add, 1024.0, ALU.mult)
+    ts([v_oh], C(7), OH(2), OH(3), ALU.add, BIG, ALU.mult)
+    ts([v_oh], C(11), OH(13), 16.0, ALU.mult)
+    ts([v_oh], C(10), OH(12), OH(13), ALU.add)
+    c1 = ts([v_oh], C(8), OH(5), 4095.0, ALU.mult, -1.0, ALU.add)
+    ts([c1], C(16), OH(2), 2.0, ALU.mult, C(6), ALU.add)
+    ts([c1], C(14), C(7), OH(0), ALU.add, OH(1), ALU.add)
+    c2 = ts([c1], C(9), C(2), 2.0, ALU.mult, C(8), ALU.add)
+    ts([c2], C(17), C(16), C(13), ALU.subtract)
+    cols = ts([c2], C(15), C(9), C(7), ALU.add)
+
+    g_l = sel([a_one], T.lb[:], T.ones[:, 0:128], [[-16, 8], [0, 16]], ALU.is_equal, -2)
+    g_id = sel([a_one], T.idf[:], T.ones[:, 0:128], [[-1, 128]], ALU.is_equal, 0)
+    g_kd = sel([a_one], T.kdl[0:8, :], T.ones[0:8, 0:128], [[-1, 8], [1000, 16]], ALU.is_equal, -13000)
+    for k in range(4):
+        a_l = act([g_l], T.lk[:, 128 * k:128 * k + 128], T.lb[:], float(16 << k))
+    g_z = sel([a_one], T.z0[:], T.ones[:], [[-16, 9], [1000, 16]], ALU.is_ge, -15000)
+    g_z = sel([g_z], T.z0[:], T.z0[:], [[16, 9], [0, 16]], ALU.is_ge, 15, -1)
+    g_l12 = sel([a_l], T.lk[:, 512:1024], T.lk[:, 0:512], [[0, 32], [1, 16]], ALU.is_equal, -12, 0)
+    g_dump = iota(T.dump[:], [[16, 32]], NA + 1, 1)
+    g_pz = iota(T.pk[:], [[0, 768]], 0, 0)
+    fill(T.CH[:, 0:PAD], PAD, 0.0)
+    fill(T.CH[:, TOP:TOP + 16], 16, 0.0)
+    fill(T.VC[:, 0:PAD], PAD, 0.0)
+    fill(T.TAB[:, 0:16], 16, -1.0)
+    fill(T.S[:, 0:256], 256, 0.0)
+    a_fill = fill(T.S[:, 256:264], 8, 0.0)
+    for k in range(2):
+        a_keep = act([v_keep], T.keep[:, 256 * k:256 * k + 256], T.cm[:], 0.0, C(13))
+    shifts = [(0, 0), (0, 1), (1, 1), (1, 2), (2, 2), (2, 3)]
+    for i, (k, c) in enumerate(shifts):
+        sh = 12 * c - 16 * k
+        r0, r1 = max(0, sh), min(16, 12 + sh)
+        g_pk = sel([g_pz, a_one], T.pk[:, i, :, r0:r1], T.ones[:, 0:8 * (r1 - r0)], [[-16, 8], [-1, r1 - r0]],
+                   ALU.is_equal, sh - r0)
+
+    def gw(lst, lo, hi):
+        return T.W[:].indirect(lst[:, lo // 16:hi // 16])
+
+    def case_mm(bank, deps, k, src, start, stop):
+        o = 512 * bank + 128 * k
+        return mm(deps, P[bank][:], T.lk[:, o:o + 128], src[:, 512 * k:512 * k + 512], start, stop, mark=stop)
+
+    mm([v_kd, g_kd], P[1][:], T.kdl[0:8, :], T.kdb[0:8, :], True, False, mark=False)
+    for c in range(4):
+        mm([v_ce, g_id], P[1][:, c::4], T.cep[:, 8 * c:8 * c + 8, :], T.idf[:], False, False, mark=False)
+    for k in range(3):
+        s = slice(512 * k, 512 * k + 512)
+        a_g = act(Wt + [v_cor], T.GA[:, s], gw(T.coru, 512 * k, 512 * k + 512), 0.0625, 0.53125)
+        v_g = tt(Wt + [a_g], T.GV[:, s], gw(T.coru, 2048 + 512 * k, 2560 + 512 * k), T.GA[:, s], ALU.add)
+        case_mm(0, [v_g, a_l], k, T.GV, k == 0, False)
+        if k == 0:
+            v_bl = cp([l_bl], T.blu[:], T.bli[:])
+        if k < 2:
+            case_mm(1, [g_l12], k, T.GV, False, False)
+    v_ea = cp([l_ea], T.eau[:], T.eai[:])
+    a_g = act([], T.GA[:, 1536:2048], gw(T.coru, 1536, 2048), 0.0625, 0.03125)
+    case_mm(0, [a_g], 3, T.GA, False, False)
+    a_g = act([], T.GV[:, 1536:2048], gw(T.coru, 3584, 4096), 1.0, 0.5)
+    p_case = case_mm(0, [a_g], 3, T.GV, False, True)
+    case_mm(1, [], 2, T.GV, False, False)
+    case_mm(1, [], 3, T.GA, False, False)
+    p_cev = case_mm(1, [], 3, T.GV, False, True)
+
+    def first_end(lo, hi):
+        return act([v_ea, cols], T.UE[:, lo:hi], gw(T.eau, lo, hi), C(2))
+
+    def second_end(lo, hi, t):
+        return tt([v_eb, t], T.X[:, lo:hi], gw(T.ebu, lo, hi), T.UE[:, lo:hi], ALU.add)
+
+    ch = [(CUTS[i], CUTS[i + 1]) for i in range(len(CUTS) - 1)]
+    ue = [first_end(*ch[0])]
+    for a, b in blocks:
+        a_T = act(Wt + [v_bl, v_oh], T.X[:, NV + NB * a:NV + NB * b], gw(T.blu, NB * a, NB * b), 1.0, OH(5))
+    sentS, arrS = send([a_T], T.X, T.MS, NV, 0, "arrS", "sentS")
+    ue.append(first_end(*ch[1]))
+    a_cev = act([p_cev, cols], T.cev[:], P[1][:], 1.0, C(11))
+    ue.append(first_end(*ch[2]))
+    v_eb = cp([l_eb], T.ebu[:], T.ebi[:])
+    v_zq = ts([g_z, cols], T.zq[:], T.z0[:], C(17), ALU.mult)
+    v_tb = cp([l_tb], T.tbb[:], T.tbi[:])
+    l_tab = dma("S", [v_tb, a_fill], [(T.TAB[16 * j:16 * j + 16, 16:16 + NV], T.tbb[:]) for j in range(8)])
+    x_b = dma("S", [sentS, arrS, a_fill] + Wt,
+              [(T.X[3::16, NV + NB * a:NV + NB * b], T.MS[2::16, NB * a:NB * b]) for a, b in blocks] +
+              [(T.X[10::16, NV:], T.W[8::16, 0:N * NB]), (T.X[11::16, NV:], T.W[9::16, 0:N * NB])])
+    v_e = ts([p_case, cols], T.ee[:], P[0][:], C(5), ALU.is_equal, OH(2), ALU.max)
+    v_sc = op("V", [v_e, a_keep], lambda e: e.tensor_tensor_scan(T.cum[:], T.keep[:], T.ee[:], 0.0, ALU.mult, ALU.add))
+    p_q = extract([v_sc, v_zq], P[2][:, 0:32], T.zq, T.cum, 0, 512)
+    second_end(*ch[0], ue[0])
+    second_end(*ch[1], ue[1])
+    v_t = tt([p_q, g_dump], T.tf[:], P[2][:, 0:32], T.dump[:], ALU.min)
+    v_t = cp([v_t], T.tu[:], T.tf[:])
+    v_S = cp([v_t, a_cev, a_fill], T.S[:].indirect(T.tu[:]), T.cev[:])
+    for i, (k, c) in enumerate(shifts):
+        p_pk = mm([v_S, g_pk], P[3][:, k:192:3], T.pk[:, i], T.S[:, 1 + c:1 + NA:4], i % 2 == 0, i % 2 == 1,
+                  mark=(i == 5))
+    ue.append(first_end(*ch[3]))
+    for a, b in blocks:
+        a_mc = act([l_ch, v_bl], T.MC[:, NB * a:NB * b], T.CH[:, PAD:PAD + NV].indirect(T.blu[:, 16 * a:16 * b]))
+    sentC, arrC = send([a_mc], T.MC, T.CH, 0, PAD + NV, "arrC", "sentC")
+    act([g_z], T.zk[:], T.z0[:], C(10))
+    a_sb = act([v_S], T.sb[:], T.S[:, 1:1 + NA])
+    for k in range(4, len(ch)):
+        ue.append(first_end(*ch[k]))
+    act([g_z], T.za[:], T.z0[:], C(15))
+    act([g_z], T.zv[:], T.z0[:], C(14))
+    a_zz = act([g_id], T.idb[:], T.idf[:])
+    p_kc = extract([a_sb], P[4][:, 0:16], T.zk, T.sb, 0, NA)
+    mm([g_cm], P[5][:, 0:NA], T.idf[:], T.cm[:], True, False, mark=False)
+    for k in range(2, len(ch)):
+        v_x = second_end(*ch[k], ue[k])
+        if k == 3:
+            v_cel = cp([p_pk], T.cel[:], P[3][:, 0:192])
+        if k == len(ch) - 3:
+            v_kc = cp([p_kc], T.kcu[:], P[4][:, 0:16])
+    x_parts = [x_b, v_x, v_cel, a_fill]
+
+    xl, pa, pv, va, vv, ca, vc = {}, {}, {}, {}, {}, {}, []
+    last = {0: v_e, 1: a_cev, 2: v_t, 3: v_cel}
+    v_yl = None
+    for step in ORDER:
+        kind, c = step[0], int(step[1])
+        if kind in "xelmav":
+            c0, c1 = CC[c], CC[c + 1]
+            ba, bv = BANKS[c]
+        if kind == "x":
+            xl[c] = []
+            cm = c0 + XA[c]
+            if cm > c0:
+                xl[c].append(act(x_parts, T.XL[:, 16 * c0:16 * cm], T.X[:].indirect(T.cel[:, c0:cm])))
+            if c1 > cm:
+                xl[c].append(cp(x_parts, T.XL[:, 16 * cm:16 * c1], T.X[:].indirect(T.cel[:, cm:c1])))
+        elif kind == "e":
+            pa[c] = extract(xl[c] + [last.get(ba), a_zz], P[ba][:, 0:c1 - c0], T.za, T.XL, 16 * c0, 16 * c1)
+            pv[c] = extract(xl[c] + [last.get(bv), a_zz], P[bv][:, 0:c1 - c0], T.zv, T.XL, 16 * c0, 16 * c1)
+        elif kind == "l":
+            va[c] = last[ba] = ts([pa[c]], T.al[:, c0:c1], P[ba][:, 0:c1 - c0], 0.0, ALU.max, float(TOP), ALU.min)
+        elif kind == "m":
+            vv[c] = last[bv] = ts([pv[c]], T.vl[:, c0:c1], P[bv][:, 0:c1 - c0], 0.0, ALU.max, float(TOP), ALU.min)
+        elif kind in "av":
+            h, half = int(step[2]), (c1 - c0) // 2
+            lo, hi = c0 + half * h, c0 + half * h + half
+            if kind == "a":
+                ca[c, h] = act([va[c], arrC, l_ch, a_fill], T.CA[:, 16 * lo:16 * hi], T.CH[:].indirect(T.al[:, lo:hi]))
+            else:
+                vc.append((16 * hi, tt([vv[c], arrC, l_ch, ca[c, h]], T.VC[:, PAD + 16 * lo:PAD + 16 * hi],
+                                       T.CH[:].indirect(T.vl[:, lo:hi]), T.CA[:, 16 * lo:16 * hi], ALU.add)))
+        elif kind == "k":
+            a_tt = act([v_kc, a_fill, l_tab], T.tt[:], T.TAB[:].indirect(T.kcu[:]), -1.0)
+            a_tn = act([a_tt], T.tn[:], T.tt[:], BIG, 0.0, RELU)
+            mm([a_tt, a_zz], P[5][:, 0:NA], T.idb[:], T.tt[:], False, False, mark=False)
+            p_y = mm([a_tn], P[5][:, 0:NA], T.idb[:], T.tn[:], False, True)
+        elif kind == "y":
+            v_yl = ts([p_y], T.yl[:], P[5][:, 0:NA], -1.0, ALU.mult, 0.0, ALU.max)
+        else:
+            m0, m1 = YS[c]
+            n, t = [x for x in vc if x[0] >= 12 * m1][0]
+            w = T.VC[:, 0:PAD + n].indirect(T.yl[:, m0:m1])
+            o = T.Y[:, 16 * m0:16 * m1]
+            t = act([v_yl, t, a_fill], o, w) if YQ[c] == "A" else cp([v_yl, t, a_fill], o, w)
+            dma("S", [t], [(T.y[:, 16 * m0:16 * m1], o)])
+
+    wait("G", [(s, n) for s, n in cnt.items()])

@@ -8,14 +8,15 @@ NV, NB, NA = 4096, 256, 256
 PAD = 16
 TOP = PAD + NV + 4 * NB
 BIG = 8192.0
-CUTS = [0, 512, 1024, 1792, 2560, 3328, 3840, 4096]
-CC = [0, 48, 96, 144, 192]
-XA = [16, 32, 20, 32]
-BANKS = [(6, 7), (0, 1), (2, 3), (6, 7)]
-YS = [(0, 28), (28, 64), (64, 96), (96, 120), (120, 142), (142, 192), (192, 222), (222, 240), (240, 256)]
-YQ = "VAAVAVAAV"
-ORDER = ("k0 x0 y0 x1 e0 e1 l0 x2 m0 a00 e2 x3 v00 e3 l1 a01 o0 v01 a10 m1 v10 a11 l2 o1 o2 a20 v11 m2 a21 o3 l3 v20 "
-         "o4 a30 v21 m3 o5 v30 a31 o6 v31 o7 o8").split()
+CUTS = [0, 768, 896, 1920, 2176, 3456, 3584, 4096]
+FIRST = "g0 h0 B E g1 h1 g2 A a3 b3 u0 h2 T D Z u1 e w0 w1 c u2 s u5 u3 w2 u4 w3 u6 S w4 M K w5 L w6".split()
+CC = [0, 56, 120, 192]
+XA = [28, 20, 40]
+BANKS = [(6, 7), (0, 1), (2, 3)]
+YS = [(0, 26), (26, 74), (74, 122), (122, 160), (160, 196), (196, 236), (236, 256)]
+YQ = "VAVAAAV"
+ORDER = ("k0 x0 y0 e0 x1 e1 l0 x2 a00 a01 m0 e2 v00 l1 o0 m1 a10 v01 a11 v10 l2 o1 v11 m2 a20 o2 v20 a21 o3 o4 v21 "
+         "o6 o5").split()
 
 F, B, I, U, H = "float32", "bfloat16", "int32", "uint16", "float16"
 SCRATCH = {
@@ -33,13 +34,12 @@ SCRATCH = {
     "cei": ("sbuf", [128, 32, 12], I), "cep": ("sbuf", [128, 32, 16], F),
     "pi": ("sbuf", [128, 48], I), "col": ("sbuf", [128, 64], F),
     "jj": ("sbuf", [128, 64], F), "mk": ("sbuf", [128, 64], F), "oh": ("sbuf", [128, 16], F),
-    "ones": ("sbuf", [128, 144], F), "lb": ("sbuf", [128, 128], F), "lk": ("sbuf", [128, 1024], B),
+    "ones": ("sbuf", [128, 144], F), "lb": ("sbuf", [128, 128], F), "lk": ("sbuf", [128, 512], B),
     "idf": ("sbuf", [128, 128], F), "idb": ("sbuf", [128, 128], B),
-    "z0": ("sbuf", [128, 144], F), "zq": ("sbuf", [128, 144], H), "za": ("sbuf", [128, 144], B),
-    "zv": ("sbuf", [128, 144], B), "zk": ("sbuf", [128, 144], B),
+    "z0": ("sbuf", [128, 144], F), "zq": ("sbuf", [128, 144], H), "zz": ("sbuf", [128, 576], B),
     "kdl": ("sbuf", [128, 128], B), "pk": ("sbuf", [128, 6, 8, 16], F),
-    "dump": ("sbuf", [128, 32], F), "cm": ("sbuf", [128, 256], F), "keep": ("sbuf", [128, 512], B),
-    "ee": ("sbuf", [128, 512], H), "cum": ("sbuf", [128, 512], H),
+    "dump": ("sbuf", [128, 32], F), "cm": ("sbuf", [128, 256], F),
+    "ee": ("sbuf", [128, 512], B), "cum": ("sbuf", [128, 512], H),
     "tf": ("sbuf", [128, 32], F), "tu": ("sbuf", [128, 32], U),
     "cev": ("sbuf", [128, 512], F), "S": ("sbuf", [128, 896], F),
     "cel": ("sbuf", [128, 192], U), "kcu": ("sbuf", [128, 16], U),
@@ -123,18 +123,19 @@ def rank_program(g, core, T, topo):
     def mm(deps, o, l, r, start, stop, mark=True):
         return op("P", deps, lambda e: e.matmul(o, l, r, start, stop), mark)
 
-    def sel(deps, o, i, pat, cmp, base, cm=1):
-        return op("G", deps, lambda e: e.affine_select(o, i, pat, cmp, 0.0, base, cm))
+    def sel(deps, o, i, pat, cmp, base, cm=1, fill=0.0):
+        return op("G", deps, lambda e: e.affine_select(o, i, pat, cmp, fill, base, cm))
 
     def iota(o, pat, base, cm, fl=True):
         if fl:
             return op("G", [], lambda e: e.iota(o, pat, base, cm, allow_small_or_imprecise_dtypes=True))
         return op("G", [], lambda e: e.iota(o, pat, base, cm))
 
-    def extract(deps, o, z, src, lo, hi):
+    def extract(deps, o, z, src, lo, hi, z0=0, start=True, stop=True):
         t = None
         for u in range(16):
-            t = mm(deps, o, z[:, 15 - u:143 - u], src[:, lo + u:hi:16], u == 0, u == 15, mark=(u == 15))
+            t = mm(deps, o, z[:, z0 + 15 - u:z0 + 143 - u], src[:, lo + u:hi:16], start and u == 0, stop and u == 15,
+                   mark=(stop and u == 15))
         return t
 
     others = [T.cores[q] for q in peers]
@@ -163,7 +164,8 @@ def rank_program(g, core, T, topo):
     l_lv = dma("S", [], [(T.lvc[:], T.lv[:])])
     l_cor = dma("S", [], [(T.cori[:], T.cor[:])])
     l_kd = dma("S", [], [(T.kdi[0:8, :], T.kd[:])])
-    l_ce = dma("S", [], [(T.cei[:, 4 * k:4 * k + 4, :], T.ce[k]) for k in range(8)])
+    l_ce = [dma(q, [], [(T.cei[:, 4 * k:4 * k + 4, :], T.ce[k]) for k in range(k0, k0 + 4)])
+            for q, k0 in (("A", 0), ("S", 4))]
 
     g_p = iota(T.pi[:, 0:16], [[-1, 16]], 16, 1, False)
     g_j = iota(T.jj[:], [[1, 64]], 0, 0)
@@ -199,31 +201,30 @@ def rank_program(g, core, T, topo):
 
     v_oh = ts([v_a], T.oh[:], T.pi[:, 32:48], 0.0, ALU.is_equal)
     v_cor = cp([l_cor], T.coru[:], T.cori[:])
-    v_kd = ts([l_kd], T.kdb[0:8, :], T.kdi[0:8, :], 256.0, ALU.mult)
-    ts([v_a], C(2), T.pi[:, 32:33], 2.0, ALU.is_ge)
-    ts([v_a], C(5), T.pi[:, 32:33], 2.0, ALU.is_ge, 255.0, ALU.mult)
-    v_keep = ts([v_oh], C(13), OH(1), OH(2), ALU.add, OH(3), ALU.add)
+    v_kd = ts([l_kd], T.kdb[0:8, :], T.kdi[0:8, :], 256.0, ALU.mult, 16.0, ALU.add)
     for c in range(4):
-        v_ce = cp([l_ce, a_cz], T.cep[:, 8 * c:8 * c + 8, 0:12], T.cei[:, c::4, :])
-    ts([v_oh], C(6), OH(0), OH(4), ALU.add, 1024.0, ALU.mult)
-    ts([v_oh], C(7), OH(2), OH(3), ALU.add, BIG, ALU.mult)
-    ts([v_oh], C(11), OH(13), 16.0, ALU.mult)
-    ts([v_oh], C(10), OH(12), OH(13), ALU.add)
-    c1 = ts([v_oh], C(8), OH(5), 4095.0, ALU.mult, -1.0, ALU.add)
-    ts([c1], C(16), OH(2), 2.0, ALU.mult, C(6), ALU.add)
-    ts([c1], C(14), C(7), OH(0), ALU.add, OH(1), ALU.add)
-    c2 = ts([c1], C(9), C(2), 2.0, ALU.mult, C(8), ALU.add)
-    ts([c2], C(17), C(16), C(13), ALU.subtract)
-    cols = ts([c2], C(15), C(9), C(7), ALU.add)
+        v_ce = cp(l_ce + [a_cz], T.cep[:, 8 * c:8 * c + 8, 0:12], T.cei[:, c::4, :])
+    ts([v_a], C(2), T.pi[:, 32:33], 2.0, ALU.is_ge)
+    cols = ts([v_oh], C(5), OH(13), 255.0, ALU.mult)
 
-    g_l = sel([a_one], T.lb[:], T.ones[:, 0:128], [[-16, 8], [0, 16]], ALU.is_equal, -2)
+    def coef(deps, ap, row, val):
+        return sel(deps, ap, ap, [[-16, 9]], ALU.not_equal, -row, 1, val)
+
+    g_l = iota(T.lb[:], [[0, 128]], 0, 0)
+    g_l = sel([a_one, g_l], T.lb[:, 12::16], T.ones[:, 0:8], [[-16, 8]], ALU.is_equal, -2)
+    g_l = sel([], T.lb[:, 13::16], T.ones[:, 0:8], [[-16, 8]], ALU.is_equal, -2)
+    g_l = sel([], T.lb[:, 14::16], T.ones[:, 0:8], [[-16, 8]], ALU.is_equal, -2)
     g_id = sel([a_one], T.idf[:], T.ones[:, 0:128], [[-1, 128]], ALU.is_equal, 0)
-    g_kd = sel([a_one], T.kdl[0:8, :], T.ones[0:8, 0:128], [[-1, 8], [1000, 16]], ALU.is_equal, -13000)
+    g_kd = sel([a_one], T.kdl[0:8, :], T.ones[0:8, 0:128], [[-1, 8], [1000, 16]], ALU.is_equal, -15000)
     for k in range(4):
         a_l = act([g_l], T.lk[:, 128 * k:128 * k + 128], T.lb[:], float(16 << k))
-    g_z = sel([a_one], T.z0[:], T.ones[:], [[-16, 9], [1000, 16]], ALU.is_ge, -15000)
-    g_z = sel([g_z], T.z0[:], T.z0[:], [[16, 9], [0, 16]], ALU.is_ge, 15, -1)
-    g_l12 = sel([a_l], T.lk[:, 512:1024], T.lk[:, 0:512], [[0, 32], [1, 16]], ALU.is_equal, -12, 0)
+    iota(T.z0[:], [[0, 144]], 0, 0)
+    t = iota(T.zz[:], [[0, 576]], 0, 0)
+    ZP, ZK, ZA, ZV = 0, 144, 288, 432
+    for row in (12, 13):
+        coef([t], T.z0[:, 15::16], row, -1.0)
+        t = coef([t], T.zz[:, ZP + 15:ZP + 144:16], row, 1024.0)
+    g_z = coef([t], T.z0[:, 15::16], 11, 1.0)
     g_dump = iota(T.dump[:], [[16, 32]], NA + 1, 1)
     g_pz = iota(T.pk[:], [[0, 768]], 0, 0)
     fill(T.CH[:, 0:PAD], PAD, 0.0)
@@ -232,8 +233,6 @@ def rank_program(g, core, T, topo):
     fill(T.TAB[:, 0:16], 16, -1.0)
     fill(T.S[:, 0:256], 256, 0.0)
     a_fill = fill(T.S[:, 256:264], 8, 0.0)
-    for k in range(2):
-        a_keep = act([v_keep], T.keep[:, 256 * k:256 * k + 256], T.cm[:], 0.0, C(13))
     shifts = [(0, 0), (0, 1), (1, 1), (1, 2), (2, 2), (2, 3)]
     for i, (k, c) in enumerate(shifts):
         sh = 12 * c - 16 * k
@@ -244,86 +243,97 @@ def rank_program(g, core, T, topo):
     def gw(lst, lo, hi):
         return T.W[:].indirect(lst[:, lo // 16:hi // 16])
 
-    def case_mm(bank, deps, k, src, start, stop):
-        o = 512 * bank + 128 * k
-        return mm(deps, P[bank][:], T.lk[:, o:o + 128], src[:, 512 * k:512 * k + 512], start, stop, mark=stop)
+    def case_mm(deps, k, src, stop):
+        return mm(deps, P[0][:], T.lk[:, 128 * k:128 * k + 128], src[:, 512 * k:512 * k + 512], False, stop, mark=stop)
 
-    mm([v_kd, g_kd], P[1][:], T.kdl[0:8, :], T.kdb[0:8, :], True, False, mark=False)
+    mm([v_kd, g_kd], P[0][:], T.kdl[0:8, :], T.kdb[0:8, :], True, False, mark=False)
     for c in range(4):
-        mm([v_ce, g_id], P[1][:, c::4], T.cep[:, 8 * c:8 * c + 8, :], T.idf[:], False, False, mark=False)
-    for k in range(3):
-        s = slice(512 * k, 512 * k + 512)
-        a_g = act(Wt + [v_cor], T.GA[:, s], gw(T.coru, 512 * k, 512 * k + 512), 0.0625, 0.53125)
-        v_g = tt(Wt + [a_g], T.GV[:, s], gw(T.coru, 2048 + 512 * k, 2560 + 512 * k), T.GA[:, s], ALU.add)
-        case_mm(0, [v_g, a_l], k, T.GV, k == 0, False)
-        if k == 0:
-            v_bl = cp([l_bl], T.blu[:], T.bli[:])
-        if k < 2:
-            case_mm(1, [g_l12], k, T.GV, False, False)
-    v_ea = cp([l_ea], T.eau[:], T.eai[:])
-    a_g = act([], T.GA[:, 1536:2048], gw(T.coru, 1536, 2048), 0.0625, 0.03125)
-    case_mm(0, [a_g], 3, T.GA, False, False)
-    a_g = act([], T.GV[:, 1536:2048], gw(T.coru, 3584, 4096), 1.0, 0.5)
-    p_case = case_mm(0, [a_g], 3, T.GV, False, True)
-    case_mm(1, [], 2, T.GV, False, False)
-    case_mm(1, [], 3, T.GA, False, False)
-    p_cev = case_mm(1, [], 3, T.GV, False, True)
-
-    def first_end(lo, hi):
-        return act([v_ea, cols], T.UE[:, lo:hi], gw(T.eau, lo, hi), C(2))
-
-    def second_end(lo, hi, t):
-        return tt([v_eb, t], T.X[:, lo:hi], gw(T.ebu, lo, hi), T.UE[:, lo:hi], ALU.add)
+        mm([v_ce, g_id], P[0][:, c::4], T.cep[:, 8 * c:8 * c + 8, :], T.idf[:], False, False, mark=False)
 
     ch = [(CUTS[i], CUTS[i + 1]) for i in range(len(CUTS) - 1)]
-    ue = [first_end(*ch[0])]
-    for a, b in blocks:
-        a_T = act(Wt + [v_bl, v_oh], T.X[:, NV + NB * a:NV + NB * b], gw(T.blu, NB * a, NB * b), 1.0, OH(5))
-    sentS, arrS = send([a_T], T.X, T.MS, NV, 0, "arrS", "sentS")
-    ue.append(first_end(*ch[1]))
-    a_cev = act([p_cev, cols], T.cev[:], P[1][:], 1.0, C(11))
-    ue.append(first_end(*ch[2]))
-    v_eb = cp([l_eb], T.ebu[:], T.ebi[:])
-    v_zq = ts([g_z, cols], T.zq[:], T.z0[:], C(17), ALU.mult)
-    v_tb = cp([l_tb], T.tbb[:], T.tbi[:])
-    l_tab = dma("S", [v_tb, a_fill], [(T.TAB[16 * j:16 * j + 16, 16:16 + NV], T.tbb[:]) for j in range(8)])
-    x_b = dma("S", [sentS, arrS, a_fill] + Wt,
-              [(T.X[3::16, NV + NB * a:NV + NB * b], T.MS[2::16, NB * a:NB * b]) for a, b in blocks] +
-              [(T.X[10::16, NV:], T.W[8::16, 0:N * NB]), (T.X[11::16, NV:], T.W[9::16, 0:N * NB])])
-    v_e = ts([p_case, cols], T.ee[:], P[0][:], C(5), ALU.is_equal, OH(2), ALU.max)
-    v_sc = op("V", [v_e, a_keep], lambda e: e.tensor_tensor_scan(T.cum[:], T.keep[:], T.ee[:], 0.0, ALU.mult, ALU.add))
-    p_q = extract([v_sc, v_zq], P[2][:, 0:32], T.zq, T.cum, 0, 512)
-    second_end(*ch[0], ue[0])
-    second_end(*ch[1], ue[1])
-    v_t = tt([p_q, g_dump], T.tf[:], P[2][:, 0:32], T.dump[:], ALU.min)
-    v_t = cp([v_t], T.tu[:], T.tf[:])
-    v_S = cp([v_t, a_cev, a_fill], T.S[:].indirect(T.tu[:]), T.cev[:])
-    for i, (k, c) in enumerate(shifts):
-        p_pk = mm([v_S, g_pk], P[3][:, k:192:3], T.pk[:, i], T.S[:, 1 + c:1 + NA:4], i % 2 == 0, i % 2 == 1,
-                  mark=(i == 5))
-    ue.append(first_end(*ch[3]))
-    for a, b in blocks:
-        a_mc = act([l_ch, v_bl], T.MC[:, NB * a:NB * b], T.CH[:, PAD:PAD + NV].indirect(T.blu[:, 16 * a:16 * b]))
-    sentC, arrC = send([a_mc], T.MC, T.CH, 0, PAD + NV, "arrC", "sentC")
-    act([g_z], T.zk[:], T.z0[:], C(10))
-    a_sb = act([v_S], T.sb[:], T.S[:, 1:1 + NA])
-    for k in range(4, len(ch)):
-        ue.append(first_end(*ch[k]))
-    act([g_z], T.za[:], T.z0[:], C(15))
-    act([g_z], T.zv[:], T.z0[:], C(14))
-    a_zz = act([g_id], T.idb[:], T.idf[:])
-    p_kc = extract([a_sb], P[4][:, 0:16], T.zk, T.sb, 0, NA)
-    mm([g_cm], P[5][:, 0:NA], T.idf[:], T.cm[:], True, False, mark=False)
-    for k in range(2, len(ch)):
-        v_x = second_end(*ch[k], ue[k])
-        if k == 3:
-            v_cel = cp([p_pk], T.cel[:], P[3][:, 0:192])
-        if k == len(ch) - 3:
-            v_kc = cp([p_kc], T.kcu[:], P[4][:, 0:16])
+    tk = {}
+    left = len([s for s in FIRST if s[0] in "hab"])
+    for step in FIRST:
+        kind, k = step[0], int(step[1:] or 0)
+        s = slice(512 * k, 512 * k + 512)
+        if kind == "g":
+            tk[step] = act(Wt + [v_cor], T.GA[:, s], gw(T.coru, 512 * k, 512 * k + 512), 0.0625, 0.53125)
+        elif kind in "hab":
+            left -= 1
+            if kind == "h":
+                t = tt(Wt + [tk["g%d" % k]], T.GV[:, s], gw(T.coru, 2048 + 512 * k, 2560 + 512 * k), T.GA[:, s], ALU.add)
+            elif kind == "a":
+                t = act(Wt + [v_cor], T.GA[:, s], gw(T.coru, 512 * k, 512 * k + 512), 0.0625, 0.03125)
+            else:
+                t = act(Wt + [v_cor], T.GV[:, s], gw(T.coru, 2048 + 512 * k, 2560 + 512 * k), 1.0, 0.5)
+            t = case_mm([t, a_l], k, T.GA if kind == "a" else T.GV, left == 0)
+            if left == 0:
+                tk["case"] = t
+        elif kind == "B":
+            tk["B"] = cp([l_bl], T.blu[:], T.bli[:])
+        elif kind == "A":
+            tk["A"] = cp([l_ea], T.eau[:], T.eai[:])
+        elif kind == "E":
+            tk["E"] = cp([l_eb], T.ebu[:], T.ebi[:])
+        elif kind == "Z":
+            tk["Z"] = cp([g_z], T.zq[:], T.z0[:])
+        elif kind == "u":
+            lo, hi = ch[k]
+            tk[step] = act(Wt + [tk["A"], cols], T.UE[:, lo:hi], gw(T.eau, lo, hi), C(2))
+        elif kind == "w":
+            lo, hi = ch[k]
+            v_x = tt([tk["E"], tk["u%d" % k]], T.X[:, lo:hi], gw(T.ebu, lo, hi), T.UE[:, lo:hi], ALU.add)
+        elif kind == "T":
+            for a, b in blocks:
+                t = act(Wt + [tk["B"], v_oh], T.X[:, NV + NB * a:NV + NB * b], gw(T.blu, NB * a, NB * b), 1.0, OH(5))
+            sentS, arrS = send([t], T.X, T.MS, NV, 0, "arrS", "sentS")
+            za, zv, zb = T.zz[:, ZA + 15:ZA + 144:16], T.zz[:, ZV + 15:ZV + 144:16], T.zz[:, ZA + 15::16]
+            t = coef([g_pk], T.zz[:, ZK + 15:ZK + 144:16], 14, 1.0)
+            sel([], zb, T.ones[:, 0:18], [[0, 2], [-16, 9]], ALU.not_equal, -2, 1, BIG)
+            g_zk = t = coef([t], T.zz[:, ZK + 15:ZK + 144:16], 15, 1.0)
+            t = sel([t], zb, zb, [[0, 2], [-16, 9]], ALU.not_equal, -3, 1, BIG)
+            sel([t], za, za, [[-16, 9]], ALU.is_ge, -2, 1, -1.0)
+            t = sel([t], zv, zv, [[16, 9]], ALU.is_ge, 3, -1)
+            t = coef([t], za, 5, 4096.0)
+            t = sel([t], za, za, [[16, 9]], ALU.is_ge, 15, -1)
+            t = sel([t], zb, zb, [[0, 2], [-16, 9]], ALU.is_ge, 0)
+            a_zz = sel([], T.idb[:], T.ones[:, 0:128], [[-1, 128]], ALU.is_equal, 0)
+        elif kind == "D":
+            t = cp([l_tb], T.tbb[:], T.tbi[:])
+            l_tab = dma("S", [t, a_fill], [(T.TAB[16 * j:16 * j + 16, 16:16 + NV], T.tbb[:]) for j in range(8)])
+            x_b = dma("S", [sentS, arrS, a_fill] + Wt,
+                      [(T.X[3::16, NV + NB * a:NV + NB * b], T.MS[2::16, NB * a:NB * b]) for a, b in blocks] +
+                      [(T.X[10::16, NV:], T.W[8::16, 0:N * NB]), (T.X[11::16, NV:], T.W[9::16, 0:N * NB])])
+        elif kind == "e":
+            tk["e"] = t = ts([tk["case"], cols], T.ee[:], P[0][:], C(5), ALU.is_equal, OH(11), ALU.max)
+            v_sc = op("V", [t], lambda e: e.tensor_tensor_scan(T.cum[:], T.ee[:], T.ee[:], 0.0, ALU.add, ALU.max))
+            extract([t, g_z], P[2][:, 0:32], T.zz, T.ee, 0, 512, ZP, True, False)
+            tk["q"] = extract([v_sc, tk["Z"]], P[2][:, 0:32], T.zq, T.cum, 0, 512, 0, False, True)
+        elif kind == "c":
+            tk["c"] = a_cev = act([tk["e"]], T.cev[:], P[0][:])
+        elif kind == "s":
+            t = tt([tk["q"], g_dump], T.tf[:], P[2][:, 0:32], T.dump[:], ALU.min)
+            v_t = cp([t], T.tu[:], T.tf[:])
+            tk["s"] = cp([v_t, tk["c"], a_fill], T.S[:].indirect(T.tu[:]), T.cev[:])
+            for i, (j, c) in enumerate(shifts):
+                tk["pk"] = mm([tk["s"], g_pk], P[3][:, j:192:3], T.pk[:, i], T.S[:, 1 + c:1 + NA:4], i % 2 == 0,
+                              i % 2 == 1, mark=(i == 5))
+        elif kind == "M":
+            for a, b in blocks:
+                t = act([l_ch, tk["B"]], T.MC[:, NB * a:NB * b], T.CH[:, PAD:PAD + NV].indirect(T.blu[:, 16 * a:16 * b]))
+            sentC, arrC = send([t], T.MC, T.CH, 0, PAD + NV, "arrC", "sentC")
+        elif kind == "S":
+            t = act([tk["s"]], T.sb[:], T.S[:, 1:1 + NA])
+            tk["S"] = extract([t, g_zk], P[4][:, 0:16], T.zz, T.sb, 0, NA, ZK)
+            mm([g_cm], P[5][:, 0:NA], T.idf[:], T.cm[:], True, False, mark=False)
+        elif kind == "L":
+            v_cel = cp([tk["pk"]], T.cel[:], P[3][:, 0:192])
+        else:
+            v_kc = cp([tk["S"]], T.kcu[:], P[4][:, 0:16])
     x_parts = [x_b, v_x, v_cel, a_fill]
 
     xl, pa, pv, va, vv, ca, vc = {}, {}, {}, {}, {}, {}, []
-    last = {0: v_e, 1: a_cev, 2: v_t, 3: v_cel}
+    last = {0: a_cev, 2: v_t, 3: v_cel}
     v_yl = None
     for step in ORDER:
         kind, c = step[0], int(step[1])
@@ -338,8 +348,8 @@ def rank_program(g, core, T, topo):
             if c1 > cm:
                 xl[c].append(cp(x_parts, T.XL[:, 16 * cm:16 * c1], T.X[:].indirect(T.cel[:, cm:c1])))
         elif kind == "e":
-            pa[c] = extract(xl[c] + [last.get(ba), a_zz], P[ba][:, 0:c1 - c0], T.za, T.XL, 16 * c0, 16 * c1)
-            pv[c] = extract(xl[c] + [last.get(bv), a_zz], P[bv][:, 0:c1 - c0], T.zv, T.XL, 16 * c0, 16 * c1)
+            pa[c] = extract(xl[c] + [last.get(ba), a_zz], P[ba][:, 0:c1 - c0], T.zz, T.XL, 16 * c0, 16 * c1, ZA)
+            pv[c] = extract(xl[c] + [last.get(bv), a_zz], P[bv][:, 0:c1 - c0], T.zz, T.XL, 16 * c0, 16 * c1, ZV)
         elif kind == "l":
             va[c] = last[ba] = ts([pa[c]], T.al[:, c0:c1], P[ba][:, 0:c1 - c0], 0.0, ALU.max, float(TOP), ALU.min)
         elif kind == "m":

@@ -8,15 +8,19 @@ NV, NB, NA = 4096, 256, 256
 PAD = 16
 TOP = PAD + NV + 4 * NB
 BIG = 8192.0
-CUTS = [0, 768, 896, 1920, 2176, 3456, 3584, 4096]
-FIRST = "g0 h0 B E g1 h1 g2 A a3 b3 u0 h2 T D Z u1 e w0 w1 c u2 s u5 u3 w2 u4 w3 u6 S w4 M K w5 L w6".split()
-CC = [0, 56, 120, 192]
-XA = [28, 20, 40]
+SL, VO = 640, 904
+BH, BL, DF, SG, FAR, FS, MARK = 13, 14, 1, 15, 3, 2, 0
+WA = 768
+UC = [0, 384, 1344, 2560, 4096]
+CC = [0, 64, 128, 192]
 BANKS = [(6, 7), (0, 1), (2, 3)]
-YS = [(0, 26), (26, 74), (74, 122), (122, 160), (160, 196), (196, 236), (236, 256)]
-YQ = "VAVAAAV"
-ORDER = ("k0 x0 y0 e0 x1 e1 l0 x2 a00 a01 m0 e2 v00 l1 o0 m1 a10 v01 a11 v10 l2 o1 v11 m2 a20 o2 v20 a21 o3 o4 v21 "
-         "o6 o5").split()
+XC = [0, 32, 64, 114, 192]
+AC = [0, 32, 64, 96, 128, 192]
+VCUT = [0, 32, 64, 90, 128, 154, 176, 192]
+YC = [0, 40, 84, 130, 166, 204, 230, 256]
+ORDER = ("lt ld col ce n1 kd g3 TV g2 n3 en t g1 h3 g0 h2 u3A h1 n2 h0 tb u1A tab0 e tab1 pad w3 c MA xb u2A m s n4 v1A w2 "
+         "u0A z1 S L w0 x1V x0A x2V x3A E0 l0 K p0V k r0 q0 p1A E1 y q1 o0A l1 p2V p3A E2 r1 o1A q2 l2 q3 p4A r2 o3V "
+         "o2A q4 q5 o4A q6 o5V o6A").split()
 
 F, B, I, U, H = "float32", "bfloat16", "int32", "uint16", "float16"
 SCRATCH = {
@@ -24,31 +28,28 @@ SCRATCH = {
     "TAB": ("sbuf", [128, 16 + NV], B), "tbi": ("sbuf", [128, 512], I), "tbb": ("sbuf", [128, 512], B),
     "GA": ("sbuf", [128, 2048], B), "GV": ("sbuf", [128, 2048], B), "sb": ("sbuf", [128, 256], B),
     "UE": ("sbuf", [128, NV], B), "XL": ("sbuf", [128, 3072], B), "CA": ("sbuf", [128, 3072], B),
-    "VC": ("sbuf", [128, PAD + 3072], F), "Y": ("sbuf", [128, 4096], F),
+    "S": ("sbuf", [128, VO + PAD + 3072], F), "Y": ("sbuf", [128, 4096], F),
     "MS": ("sbuf", [128, 4 * NB], B), "MC": ("sbuf", [128, 4 * NB], B),
     "lvc": ("sbuf", [128, 256], B), "sc": ("sbuf", [128, 256], B),
-    "cori": ("sbuf", [128, 256], I), "eai": ("sbuf", [128, 256], I), "ebi": ("sbuf", [128, 256], I),
-    "bli": ("sbuf", [128, 64], I), "coru": ("sbuf", [128, 256], U), "eau": ("sbuf", [128, 256], U),
-    "ebu": ("sbuf", [128, 256], U), "blu": ("sbuf", [128, 64], U),
-    "kdi": ("sbuf", [128, 512], I), "kdb": ("sbuf", [128, 512], B),
+    "lo": ("sbuf", [128, 288], B), "hi": ("sbuf", [128, 256], B),
+    "cbi": ("sbuf", [128, 320], I), "cbu": ("sbuf", [128, 320], U),
+    "eni": ("sbuf", [128, 512], I), "enu": ("sbuf", [128, 512], U),
+    "kdi": ("sbuf", [128, 128], I), "kdb": ("sbuf", [128, 128], B),
     "cei": ("sbuf", [128, 32, 12], I), "cep": ("sbuf", [128, 32, 16], F),
-    "pi": ("sbuf", [128, 48], I), "col": ("sbuf", [128, 64], F),
-    "jj": ("sbuf", [128, 64], F), "mk": ("sbuf", [128, 64], F), "oh": ("sbuf", [128, 16], F),
-    "ones": ("sbuf", [128, 144], F), "lb": ("sbuf", [128, 128], F), "lk": ("sbuf", [128, 512], B),
-    "idf": ("sbuf", [128, 128], F), "idb": ("sbuf", [128, 128], B),
-    "z0": ("sbuf", [128, 144], F), "zq": ("sbuf", [128, 144], H), "zz": ("sbuf", [128, 576], B),
-    "kdl": ("sbuf", [128, 128], B), "pk": ("sbuf", [128, 6, 8, 16], F),
-    "dump": ("sbuf", [128, 32], F), "cm": ("sbuf", [128, 256], F),
+    "pi": ("sbuf", [128, 8], I), "col": ("sbuf", [128, 16], F),
+    "lb": ("sbuf", [128, 8, 16], F), "lk": ("sbuf", [128, 512], B),
+    "idf": ("sbuf", [128, 128], F), "idb": ("sbuf", [128, 128], B), "zz": ("sbuf", [128, 736], B),
+    "kdl": ("sbuf", [128, 512], B), "pk": ("sbuf", [128, 6, 8, 16], F),
+    "dump": ("sbuf", [128, 32], F), "m12": ("sbuf", [128, 128], B),
     "ee": ("sbuf", [128, 512], B), "cum": ("sbuf", [128, 512], H),
-    "tf": ("sbuf", [128, 32], F), "tu": ("sbuf", [128, 32], U),
-    "cev": ("sbuf", [128, 512], F), "S": ("sbuf", [128, 896], F),
+    "tf": ("sbuf", [128, 32], F), "tu": ("sbuf", [128, 32], U), "cev": ("sbuf", [128, 512], F),
     "cel": ("sbuf", [128, 192], U), "kcu": ("sbuf", [128, 16], U),
     "tt": ("sbuf", [128, 256], B), "tn": ("sbuf", [128, 256], B), "yl": ("sbuf", [128, 256], U),
     "al": ("sbuf", [128, 192], U), "vl": ("sbuf", [128, 192], U),
 }
 for _k in range(8):
     SCRATCH["P%d" % _k] = ("psum", [128, 512], F)
-SEMAPHORES = ["sV", "sA", "sP", "sG", "arrS", "arrC", "sentS", "sentC"] + ["d%d" % k for k in range(30)]
+SEMAPHORES = ["sV", "sA", "sP", "sG", "arrS", "arrC", "sentS", "sentC"] + ["d%d" % k for k in range(40)]
 
 
 def engine_sets(topo, src, dsts):
@@ -117,25 +118,31 @@ def rank_program(g, core, T, topo):
     def tt(deps, o, a, b, alu):
         return op("V", deps, lambda e: e.tensor_tensor(o, a, b, alu))
 
+    def mset(o, val):
+        return op("V", [], lambda e: e.memset(o, val))
+
     def act(deps, o, i, scale=1.0, bias=0.0, func=ID):
         return op("A", deps, lambda e: e.activation(o, i, func, bias=bias, scale=scale))
+
+    def lin(q, deps, o, i, scale=1.0):
+        return act(deps, o, i, scale) if q == "A" else ts(deps, o, i, scale, ALU.mult)
 
     def mm(deps, o, l, r, start, stop, mark=True):
         return op("P", deps, lambda e: e.matmul(o, l, r, start, stop), mark)
 
-    def sel(deps, o, i, pat, cmp, base, cm=1, fill=0.0):
-        return op("G", deps, lambda e: e.affine_select(o, i, pat, cmp, fill, base, cm))
+    def put(deps, o, i, pat, base, val):
+        return op("G", deps, lambda e: e.affine_select(o, i, pat, ALU.not_equal, val, base, 1))
 
     def iota(o, pat, base, cm, fl=True):
         if fl:
             return op("G", [], lambda e: e.iota(o, pat, base, cm, allow_small_or_imprecise_dtypes=True))
         return op("G", [], lambda e: e.iota(o, pat, base, cm))
 
-    def extract(deps, o, z, src, lo, hi, z0=0, start=True, stop=True):
+    def extract(deps, o, src, lo, hi, z0, start=True, stop=True):
         t = None
         for u in range(16):
-            t = mm(deps, o, z[:, z0 + 15 - u:z0 + 143 - u], src[:, lo + u:hi:16], start and u == 0, stop and u == 15,
-                   mark=(stop and u == 15))
+            t = mm(deps, o, T.zz[:, z0 + 15 - u:z0 + 143 - u], src[:, lo + u:hi:16], start and u == 0,
+                   stop and u == 15, mark=(stop and u == 15))
         return t
 
     others = [T.cores[q] for q in peers]
@@ -157,224 +164,222 @@ def rank_program(g, core, T, topo):
         return (sent, n_out), (arr, n_in)
 
     C = lambda k: T.col[:, k:k + 1]
-    OH = lambda j: T.oh[:, j:j + 1]
     P = [T["P%d" % k] for k in range(8)]
     blocks = [b for b in [(0, rank), (rank + 1, N)] if b[1] > b[0]]
+    step = ""
 
     l_lv = dma("S", [], [(T.lvc[:], T.lv[:])])
-    l_cor = dma("S", [], [(T.cori[:], T.cor[:])])
-    l_kd = dma("S", [], [(T.kdi[0:8, :], T.kd[:])])
+    l_cb = dma("S", [], [(T.cbi[:, 0:256], T.cor[:]), (T.cbi[:, 256:320], T.bl[:])])
     l_ce = [dma(q, [], [(T.cei[:, 4 * k:4 * k + 4, :], T.ce[k]) for k in range(k0, k0 + 4)])
             for q, k0 in (("A", 0), ("S", 4))]
+    l_kd = dma("S", [], [(T.kdi[0:32, :], T.kd[:])])
 
-    g_p = iota(T.pi[:, 0:16], [[-1, 16]], 16, 1, False)
-    g_j = iota(T.jj[:], [[1, 64]], 0, 0)
-    g_cm = iota(T.cm[:], [[-12, 256]], -PAD, 0)
-    t = ts([g_p], T.pi[:, 16:18], T.pi[:, 0:2], 7, ALU.bitwise_and)
-    v_a = ts([g_p], T.pi[:, 32:48], T.pi[:, 0:16], 15, ALU.bitwise_and)
-    t = ts([t], T.col[:, 0:2], T.pi[:, 16:18], 0.0, ALU.is_equal)
-    ts([t, g_j], T.W[:, 0:64], T.jj[:], float(PAD), ALU.add, C(1), ALU.mult)
-    t = ts([t, g_j], T.mk[:], T.jj[:], 64.0, ALU.mult, C(0), ALU.mult)
-    for n in (64, 256):
-        for j in (1, 2, 3):
-            t2 = ts([t], T.W[:, n * j:n * j + n], T.W[:, 0:n], T.mk[:, n * j // 64:n * j // 64 + 1], ALU.add)
-        t = t2
+    g_hi = iota(T.col[:, 6:8], [[-PAD, 2]], 0, 256)
+    g_lo = iota(T.lo[:], [[1, 288]], 0, 0)
+    g_p = iota(T.pi[:, 0:1], [[0, 1]], 0, 1, False)
+    v_w = mset(T.W[:, 0:WA], 1.0)
+    v_w2 = mset(T.W[:, WA:NV - WA], 1.0)
+    act([v_w], T.W[:, NV - WA:], T.W[:, 0:WA])
+    a_w = act([g_lo], T.hi[:], T.lo[:, 0:256], 0.0, C(6))
+    v_s = ts([l_lv], T.sc[:], T.lvc[:], 0.0, ALU.is_lt, 0.5, ALU.subtract)
+    w_n = dma("S", [a_w, v_w2], [(T.W[BL::16, :], T.lo[:, 0:256]), (T.W[DF + 8::16, :], T.lo[:, 0:256]),
+                                 (T.W[BH::16, :], T.hi[:]), (T.W[DF::16, :], T.hi[:])])
+    w_s = dma("S", [v_s], [(T.W[SG::16, :], T.sc[:])])
+    l_en = dma("S", [], [(T.eni[:, 0:256], T.ea[:]), (T.eni[:, 256:512], T.eb[:])])
+    sl = PAD + NV + NB * rank
+    Wt = [w_n, w_s]
+    v_zz = mset(T.zz[:], 0.0)
+    v_cb = cp([l_cb], T.cbu[:], T.cbi[:])
 
     def fill(o, n, val):
-        return act([g_cm], o, T.cm[:, 0:n], 0.0, val)
-
-    a_one = fill(T.ones[:], 144, 1.0)
-    a_cz = fill(T.cep[:, :, 12:16], 128, 0.0)
-    fill(T.X[:, NV + NB * rank:NV + NB * rank + NB], NB, -1.0)
-    a_w = act([t], T.W[:, 3072:4096], T.W[:, 0:1024], 1.0, T.mk[:, 48:49])
-    ts([t], T.W[:, 1024:2048], T.W[:, 0:1024], T.mk[:, 16:17], ALU.add)
-    ts([l_lv], T.sc[:], T.lvc[:], 0.0, ALU.is_lt, 0.5, ALU.subtract)
-    v_s = ts([t], T.W[:, 2048:3072], T.W[:, 0:1024], T.mk[:, 32:33], ALU.add)
-    w_s = dma("S", [a_w, v_s], [(T.W[2::16, :], T.sc[:])])
-    l_bl = dma("S", [], [(T.bli[:], T.bl[:])])
-    l_ea = dma("S", [], [(T.eai[:], T.ea[:])])
-    l_eb = dma("S", [], [(T.ebi[:], T.eb[:])])
-    l_tb = dma("S", [], [(T.tbi[:], T.tab[:])])
-    sl = PAD + NV + NB * rank
-    l_ch = dma("S", [], [(T.CH[:, PAD:PAD + NV], T.ch[:]), (T.CH[:, sl:sl + NB], T.ch[:, 0:NB])])
-    Wt = [w_s]
-
-    v_oh = ts([v_a], T.oh[:], T.pi[:, 32:48], 0.0, ALU.is_equal)
-    v_cor = cp([l_cor], T.coru[:], T.cori[:])
-    v_kd = ts([l_kd], T.kdb[0:8, :], T.kdi[0:8, :], 256.0, ALU.mult, 16.0, ALU.add)
-    for c in range(4):
-        v_ce = cp(l_ce + [a_cz], T.cep[:, 8 * c:8 * c + 8, 0:12], T.cei[:, c::4, :])
-    ts([v_a], C(2), T.pi[:, 32:33], 2.0, ALU.is_ge)
-    cols = ts([v_oh], C(5), OH(13), 255.0, ALU.mult)
+        return act([g_lo], o, T.lo[:, 0:n], 0.0, val)
 
     def coef(deps, ap, row, val):
-        return sel(deps, ap, ap, [[-16, 9]], ALU.not_equal, -row, 1, val)
+        return put(deps, ap, ap, [[-16, 9]], -row, val)
 
-    g_l = iota(T.lb[:], [[0, 128]], 0, 0)
-    g_l = sel([a_one, g_l], T.lb[:, 12::16], T.ones[:, 0:8], [[-16, 8]], ALU.is_equal, -2)
-    g_l = sel([], T.lb[:, 13::16], T.ones[:, 0:8], [[-16, 8]], ALU.is_equal, -2)
-    g_l = sel([], T.lb[:, 14::16], T.ones[:, 0:8], [[-16, 8]], ALU.is_equal, -2)
-    g_id = sel([a_one], T.idf[:], T.ones[:, 0:128], [[-1, 128]], ALU.is_equal, 0)
-    g_kd = sel([a_one], T.kdl[0:8, :], T.ones[0:8, 0:128], [[-1, 8], [1000, 16]], ALU.is_equal, -15000)
+    t = iota(T.lb[:], [[0, 128]], 0, 0)
+    g_id = put([t], T.idf[:], T.lb[:], [[-1, 128]], 0, 1.0)
+    put([g_id], T.lb[:, :, 12:16:2], T.lb[:, :, 12:16:2], [[-16, 8], [0, 2]], -SG, 1.0)
+    g_lb = put([], T.lb[:, :, 13], T.lb[:, :, 13], [[-16, 8]], -SG, -1.0)
+    g_kd = put([v_zz], T.kdl[0:32, :], T.zz[0:32, 0:512], [[-1, 4], [-4, 8], [1000, 16]], -15000, 1.0)
+    a_cz = fill(T.cep[:, :, 12:16], 128, 0.0)
     for k in range(4):
-        a_l = act([g_l], T.lk[:, 128 * k:128 * k + 128], T.lb[:], float(16 << k))
-    iota(T.z0[:], [[0, 144]], 0, 0)
-    t = iota(T.zz[:], [[0, 576]], 0, 0)
-    ZP, ZK, ZA, ZV = 0, 144, 288, 432
-    for row in (12, 13):
-        coef([t], T.z0[:, 15::16], row, -1.0)
-        t = coef([t], T.zz[:, ZP + 15:ZP + 144:16], row, 1024.0)
-    g_z = coef([t], T.z0[:, 15::16], 11, 1.0)
-    g_dump = iota(T.dump[:], [[16, 32]], NA + 1, 1)
-    g_pz = iota(T.pk[:], [[0, 768]], 0, 0)
-    fill(T.CH[:, 0:PAD], PAD, 0.0)
-    fill(T.CH[:, TOP:TOP + 16], 16, 0.0)
-    fill(T.VC[:, 0:PAD], PAD, 0.0)
-    fill(T.TAB[:, 0:16], 16, -1.0)
-    fill(T.S[:, 0:256], 256, 0.0)
-    a_fill = fill(T.S[:, 256:264], 8, 0.0)
+        a_l = act([g_lb], T.lk[:, 128 * k:128 * k + 128], T.lb[:], float(16 << k))
+    fill(T.X[:, NV + NB * rank:NV + NB * rank + NB], NB, -1.0)
+    act([], T.m12[0:1, :], T.lo[0:1, 0:128], 0.0, -12.0)
+    act([g_id], T.idb[:], T.idf[:])
+    a_fill = fill(T.S[:, SL:VO + PAD], VO + PAD - SL, 0.0)
+    ZP, ZQ, ZK, ZA, ZV, ZERO = 0, 144, 288, 432, 576, T.zz[:, 720:736]
+    Z = lambda z: T.zz[:, z + 15:z + 144:16]
     shifts = [(0, 0), (0, 1), (1, 1), (1, 2), (2, 2), (2, 3)]
-    for i, (k, c) in enumerate(shifts):
-        sh = 12 * c - 16 * k
-        r0, r1 = max(0, sh), min(16, 12 + sh)
-        g_pk = sel([g_pz, a_one], T.pk[:, i, :, r0:r1], T.ones[:, 0:8 * (r1 - r0)], [[-16, 8], [-1, r1 - r0]],
-                   ALU.is_equal, sh - r0)
 
     def gw(lst, lo, hi):
         return T.W[:].indirect(lst[:, lo // 16:hi // 16])
 
-    def case_mm(deps, k, src, stop):
-        return mm(deps, P[0][:], T.lk[:, 128 * k:128 * k + 128], src[:, 512 * k:512 * k + 512], False, stop, mark=stop)
+    def upto(done, cuts, hi):
+        return [done[k] for k in range(len(cuts) - 1) if cuts[k] < hi]
 
-    mm([v_kd, g_kd], P[0][:], T.kdl[0:8, :], T.kdb[0:8, :], True, False, mark=False)
-    for c in range(4):
-        mm([v_ce, g_id], P[0][:, c::4], T.cep[:, 8 * c:8 * c + 8, :], T.idf[:], False, False, mark=False)
-
-    ch = [(CUTS[i], CUTS[i + 1]) for i in range(len(CUTS) - 1)]
-    tk = {}
-    left = len([s for s in FIRST if s[0] in "hab"])
-    for step in FIRST:
-        kind, k = step[0], int(step[1:] or 0)
+    into0 = [s for s in ORDER if s[0] in "hab" or s in ("ce", "kd")]
+    tk, tu, tw, tx, tp, tq, tl, tr_ = {}, {}, {}, {}, {}, {}, {}, {}
+    last = {}
+    for step in ORDER:
+        q = step[-1]
+        name = step[:-1] if len(step) > 1 and q in "AV" else step
+        kind, k = (name[:-1], int(name[-1])) if name[-1].isdigit() else (name, 0)
         s = slice(512 * k, 512 * k + 512)
         if kind == "g":
-            tk[step] = act(Wt + [v_cor], T.GA[:, s], gw(T.coru, 512 * k, 512 * k + 512), 0.0625, 0.53125)
-        elif kind in "hab":
-            left -= 1
+            tk[step] = act(Wt + [v_cb], T.GA[:, s], gw(T.cbu, 512 * k, 512 * k + 512), 0.0625)
+        elif kind in ("h", "a", "b"):
+            low, high = gw(T.cbu, 512 * k, 512 * k + 512), gw(T.cbu, 2048 + 512 * k, 2560 + 512 * k)
             if kind == "h":
-                t = tt(Wt + [tk["g%d" % k]], T.GV[:, s], gw(T.coru, 2048 + 512 * k, 2560 + 512 * k), T.GA[:, s], ALU.add)
+                t = tt(Wt + [tk["g%d" % k]], T.GV[:, s], high, T.GA[:, s], ALU.add)
             elif kind == "a":
-                t = act(Wt + [v_cor], T.GA[:, s], gw(T.coru, 512 * k, 512 * k + 512), 0.0625, 0.03125)
+                t = lin(q, Wt + [v_cb], T.GA[:, s], low, 0.0625)
             else:
-                t = act(Wt + [v_cor], T.GV[:, s], gw(T.coru, 2048 + 512 * k, 2560 + 512 * k), 1.0, 0.5)
-            t = case_mm([t, a_l], k, T.GA if kind == "a" else T.GV, left == 0)
-            if left == 0:
-                tk["case"] = t
-        elif kind == "B":
-            tk["B"] = cp([l_bl], T.blu[:], T.bli[:])
-        elif kind == "A":
-            tk["A"] = cp([l_ea], T.eau[:], T.eai[:])
-        elif kind == "E":
-            tk["E"] = cp([l_eb], T.ebu[:], T.ebi[:])
-        elif kind == "Z":
-            tk["Z"] = cp([g_z], T.zq[:], T.z0[:])
+                t = lin(q, Wt + [v_cb], T.GV[:, s], high)
+            tk["case"] = mm([t, a_l], P[0][:], T.lk[:, 128 * k:128 * k + 128], (T.GA if kind == "a" else T.GV)[:, s],
+                            step == into0[0], step == into0[-1], mark=step == into0[-1])
+        elif kind == "ce":
+            for c in range(4):
+                t = cp(l_ce + [a_cz], T.cep[:, 8 * c:8 * c + 8, 0:12], T.cei[:, c::4, :])
+                end = step == into0[-1] and c == 3
+                tk["case"] = mm([t, g_id], P[0][:, c::4], T.cep[:, 8 * c:8 * c + 8, :], T.idf[:],
+                                step == into0[0] and c == 0, end, mark=end)
+        elif kind == "kd":
+            t = ts([l_kd], T.kdb[0:32, :], T.kdi[0:32, :], 256.0, ALU.mult, 144.0, ALU.add)
+            for v in range(4):
+                end = step == into0[-1] and v == 3
+                tk["case"] = mm([t, g_kd], P[0][:, 128 * v:128 * v + 128], T.kdl[0:32, 128 * v:128 * v + 128],
+                                T.kdb[0:32, :], step == into0[0] and v == 0, end, mark=end)
+        elif kind == "col":
+            r = T.pi[:, 1:2]
+            t = ts([g_p], r, T.pi[:, 0:1], 15, ALU.bitwise_and)
+            t1 = ts([t], C(1), r, float(BH), ALU.is_ge, 1.0, ALU.subtract)
+            ts([t], C(3), r, float(MARK), ALU.not_equal)
+            ts([t], C(4), r, 11.0, ALU.is_equal)
+            ts([t, g_hi], C(5), r, -256.0, ALU.mult, C(7), ALU.add)
+            tk["col"] = ts([t1], C(2), r, float(SG), ALU.is_ge, C(1), ALU.add)
+        elif kind == "en":
+            tk[kind] = cp([l_en], T.enu[:], T.eni[:])
+        elif kind == "tb":
+            tk[kind] = ts([tk["lt"]], T.tbb[:], T.tbi[:], 1.0, ALU.add)
+        elif kind == "tab":
+            tk[step] = dma("S", [tk["tb"]],
+                           [(T.TAB[16 * j:16 * j + 16, 16:16 + NV], T.tbb[:]) for j in range(4 * k, 4 * k + 4)])
+        elif kind == "n" and k == 1:
+            t = coef([g_kd], Z(ZQ), 11, 1.0)
+            t1 = coef([], Z(ZP), 11, float(SL))
+            for row in (12, 13):
+                t = coef([t], Z(ZQ), row, -1.0)
+                t1 = coef([t1], Z(ZP), row, -2048.0)
+            tk["n1"] = iota(T.dump[:], [[16, 32]], 0, 1)
+        elif kind == "n" and k == 2:
+            t = iota(T.pk[:], [[0, 768]], 0, 0)
+            for i, (j, c) in enumerate(shifts):
+                sh = 12 * c - 16 * j
+                r0, r1 = max(0, sh), min(16, 12 + sh)
+                tk["n2"] = put([t], T.pk[:, i, :, r0:r1], T.pk[:, i, :, r0:r1], [[-16, 8], [-1, r1 - r0]], sh - r0, 1.0)
+        elif kind == "n" and k == 3:
+            t = coef([g_kd], Z(ZK), 14, 1.0)
+            tk["zk"] = coef([t], Z(ZK), 15, 1.0)
+        elif kind == "n":
+            zb, t = T.zz[:, ZA + 15:720:16], g_kd
+            for row, val in ((BH, 1.0), (BL, 1.0), (SG, BIG), (FS, BIG)):
+                t = put([t], zb, zb, [[0, 2], [-16, 9]], -row, val)
+            for row, val in ((DF, -1.0), (DF + 8, -1.0), (FAR, 1.0), (FAR + 8, 1.0), (MARK, float(NV))):
+                tk["n4"] = t = coef([t], Z(ZA), row, val)
         elif kind == "u":
-            lo, hi = ch[k]
-            tk[step] = act(Wt + [tk["A"], cols], T.UE[:, lo:hi], gw(T.eau, lo, hi), C(2))
+            lo, hi = UC[k], UC[k + 1]
+            tu[k] = lin(q, Wt + [tk["en"], tk["col"]], T.UE[:, lo:hi], gw(T.enu, lo, hi),
+                        1.0 if "z%d" % k in ORDER else C(2))
+        elif kind == "v":
+            lo, hi = UC[k], UC[k + 1]
+            tk["v", k] = lin(q, Wt + [tk["en"], tk["col"]], T.X[:, lo:hi], gw(T.enu, NV + lo, NV + hi), C(3))
+        elif kind == "z":
+            lo, hi = UC[k], UC[k + 1]
+            tw[k] = dma("S", [tk["v", k], tu[k]], [(T.X[FAR::8, lo:hi], T.UE[DF::8, lo:hi]),
+                                                   (T.X[FS::16, lo:hi], T.UE[SG::16, lo:hi])])
         elif kind == "w":
-            lo, hi = ch[k]
-            v_x = tt([tk["E"], tk["u%d" % k]], T.X[:, lo:hi], gw(T.ebu, lo, hi), T.UE[:, lo:hi], ALU.add)
+            lo, hi = UC[k], UC[k + 1]
+            tw[k] = tt([tu[k]], T.X[:, lo:hi], gw(T.enu, NV + lo, NV + hi), T.UE[:, lo:hi], ALU.add)
+        elif kind == "ld":
+            tk["ch"] = dma("S", [], [(T.CH[:, PAD:PAD + NV], T.ch[:]), (T.CH[:, sl:sl + NB], T.ch[:, 0:NB])])
+        elif kind == "lt":
+            tk["lt"] = dma("S", [], [(T.tbi[:], T.tab[:])])
+        elif kind == "pad":
+            tk["pad"] = dma("S", [v_zz], [(T.CH[:, 0:PAD], ZERO), (T.CH[:, TOP:], ZERO), (T.TAB[:, 0:16], ZERO)])
         elif kind == "T":
             for a, b in blocks:
-                t = act(Wt + [tk["B"], v_oh], T.X[:, NV + NB * a:NV + NB * b], gw(T.blu, NB * a, NB * b), 1.0, OH(5))
-            sentS, arrS = send([t], T.X, T.MS, NV, 0, "arrS", "sentS")
-            za, zv, zb = T.zz[:, ZA + 15:ZA + 144:16], T.zz[:, ZV + 15:ZV + 144:16], T.zz[:, ZA + 15::16]
-            t = coef([g_pk], T.zz[:, ZK + 15:ZK + 144:16], 14, 1.0)
-            sel([], zb, T.ones[:, 0:18], [[0, 2], [-16, 9]], ALU.not_equal, -2, 1, BIG)
-            g_zk = t = coef([t], T.zz[:, ZK + 15:ZK + 144:16], 15, 1.0)
-            t = sel([t], zb, zb, [[0, 2], [-16, 9]], ALU.not_equal, -3, 1, BIG)
-            sel([t], za, za, [[-16, 9]], ALU.is_ge, -2, 1, -1.0)
-            t = sel([t], zv, zv, [[16, 9]], ALU.is_ge, 3, -1)
-            t = coef([t], za, 5, 4096.0)
-            t = sel([t], za, za, [[16, 9]], ALU.is_ge, 15, -1)
-            t = sel([t], zb, zb, [[0, 2], [-16, 9]], ALU.is_ge, 0)
-            a_zz = sel([], T.idb[:], T.ones[:, 0:128], [[-1, 128]], ALU.is_equal, 0)
-        elif kind == "D":
-            t = cp([l_tb], T.tbb[:], T.tbi[:])
-            l_tab = dma("S", [t, a_fill], [(T.TAB[16 * j:16 * j + 16, 16:16 + NV], T.tbb[:]) for j in range(8)])
-            x_b = dma("S", [sentS, arrS, a_fill] + Wt,
-                      [(T.X[3::16, NV + NB * a:NV + NB * b], T.MS[2::16, NB * a:NB * b]) for a, b in blocks] +
-                      [(T.X[10::16, NV:], T.W[8::16, 0:N * NB]), (T.X[11::16, NV:], T.W[9::16, 0:N * NB])])
-        elif kind == "e":
-            tk["e"] = t = ts([tk["case"], cols], T.ee[:], P[0][:], C(5), ALU.is_equal, OH(11), ALU.max)
-            v_sc = op("V", [t], lambda e: e.tensor_tensor_scan(T.cum[:], T.ee[:], T.ee[:], 0.0, ALU.add, ALU.max))
-            extract([t, g_z], P[2][:, 0:32], T.zz, T.ee, 0, 512, ZP, True, False)
-            tk["q"] = extract([v_sc, tk["Z"]], P[2][:, 0:32], T.zq, T.cum, 0, 512, 0, False, True)
-        elif kind == "c":
-            tk["c"] = a_cev = act([tk["e"]], T.cev[:], P[0][:])
-        elif kind == "s":
-            t = tt([tk["q"], g_dump], T.tf[:], P[2][:, 0:32], T.dump[:], ALU.min)
-            v_t = cp([t], T.tu[:], T.tf[:])
-            tk["s"] = cp([v_t, tk["c"], a_fill], T.S[:].indirect(T.tu[:]), T.cev[:])
-            for i, (j, c) in enumerate(shifts):
-                tk["pk"] = mm([tk["s"], g_pk], P[3][:, j:192:3], T.pk[:, i], T.S[:, 1 + c:1 + NA:4], i % 2 == 0,
-                              i % 2 == 1, mark=(i == 5))
+                tk["T"] = lin(q, Wt + [v_cb], T.X[:, NV + NB * a:NV + NB * b], gw(T.cbu, NV + NB * a, NV + NB * b))
+        elif kind == "t":
+            sentS, arrS = send([tk["T"]], T.X, T.MS, NV, 0, "arrS", "sentS")
+        elif kind == "xb":
+            tk["xb"] = dma("S", [sentS, arrS, a_fill] + Wt,
+                           [(T.X[FS::16, NV + NB * a:NV + NB * b], T.MS[SG::16, NB * a:NB * b]) for a, b in blocks] +
+                           [(T.X[FAR::8, NV:], T.W[DF::8, 0:N * NB])])
         elif kind == "M":
             for a, b in blocks:
-                t = act([l_ch, tk["B"]], T.MC[:, NB * a:NB * b], T.CH[:, PAD:PAD + NV].indirect(T.blu[:, 16 * a:16 * b]))
-            sentC, arrC = send([t], T.MC, T.CH, 0, PAD + NV, "arrC", "sentC")
-        elif kind == "S":
-            t = act([tk["s"]], T.sb[:], T.S[:, 1:1 + NA])
-            tk["S"] = extract([t, g_zk], P[4][:, 0:16], T.zz, T.sb, 0, NA, ZK)
-            mm([g_cm], P[5][:, 0:NA], T.idf[:], T.cm[:], True, False, mark=False)
-        elif kind == "L":
-            v_cel = cp([tk["pk"]], T.cel[:], P[3][:, 0:192])
-        else:
-            v_kc = cp([tk["S"]], T.kcu[:], P[4][:, 0:16])
-    x_parts = [x_b, v_x, v_cel, a_fill]
-
-    xl, pa, pv, va, vv, ca, vc = {}, {}, {}, {}, {}, {}, []
-    last = {0: a_cev, 2: v_t, 3: v_cel}
-    v_yl = None
-    for step in ORDER:
-        kind, c = step[0], int(step[1])
-        if kind in "xelmav":
-            c0, c1 = CC[c], CC[c + 1]
-            ba, bv = BANKS[c]
-        if kind == "x":
-            xl[c] = []
-            cm = c0 + XA[c]
-            if cm > c0:
-                xl[c].append(act(x_parts, T.XL[:, 16 * c0:16 * cm], T.X[:].indirect(T.cel[:, c0:cm])))
-            if c1 > cm:
-                xl[c].append(cp(x_parts, T.XL[:, 16 * cm:16 * c1], T.X[:].indirect(T.cel[:, cm:c1])))
-        elif kind == "e":
-            pa[c] = extract(xl[c] + [last.get(ba), a_zz], P[ba][:, 0:c1 - c0], T.zz, T.XL, 16 * c0, 16 * c1, ZA)
-            pv[c] = extract(xl[c] + [last.get(bv), a_zz], P[bv][:, 0:c1 - c0], T.zz, T.XL, 16 * c0, 16 * c1, ZV)
-        elif kind == "l":
-            va[c] = last[ba] = ts([pa[c]], T.al[:, c0:c1], P[ba][:, 0:c1 - c0], 0.0, ALU.max, float(TOP), ALU.min)
+                tk["M"] = lin(q, [tk["ch"], v_cb], T.MC[:, NB * a:NB * b],
+                              T.CH[:, PAD:PAD + NV].indirect(T.cbu[:, 256 + 16 * a:256 + 16 * b]))
         elif kind == "m":
-            vv[c] = last[bv] = ts([pv[c]], T.vl[:, c0:c1], P[bv][:, 0:c1 - c0], 0.0, ALU.max, float(TOP), ALU.min)
-        elif kind in "av":
-            h, half = int(step[2]), (c1 - c0) // 2
-            lo, hi = c0 + half * h, c0 + half * h + half
-            if kind == "a":
-                ca[c, h] = act([va[c], arrC, l_ch, a_fill], T.CA[:, 16 * lo:16 * hi], T.CH[:].indirect(T.al[:, lo:hi]))
-            else:
-                vc.append((16 * hi, tt([vv[c], arrC, l_ch, ca[c, h]], T.VC[:, PAD + 16 * lo:PAD + 16 * hi],
-                                       T.CH[:].indirect(T.vl[:, lo:hi]), T.CA[:, 16 * lo:16 * hi], ALU.add)))
+            sentC, arrC = send([tk["M"]], T.MC, T.CH, 0, PAD + NV, "arrC", "sentC")
+        elif kind == "e":
+            tk["e"] = t = ts([tk["case"], tk["col"]], T.ee[:], P[0][:], -127.5, ALU.is_equal, C(4), ALU.max)
+            v_sc = op("V", [t], lambda e: e.tensor_tensor_scan(T.cum[:], T.ee[:], T.ee[:], 0.0, ALU.add, ALU.max))
+            extract([t, tk["n1"]], P[2][:, 0:32], T.ee, 0, 512, ZP, True, False)
+            tk["q"] = extract([v_sc], P[2][:, 0:32], T.cum, 0, 512, ZQ, False, True)
+        elif kind == "c":
+            tk["c"] = last[0] = act([tk["e"]], T.cev[:], P[0][:])
+        elif kind == "s":
+            t = tt([tk["q"]], T.tf[:], P[2][:, 0:32], T.dump[:], ALU.max)
+            last[2] = t = cp([t], T.tu[:], T.tf[:])
+            tk["s"] = cp([t, tk["c"], a_fill], T.S[:, 0:VO].indirect(T.tu[:]), T.cev[:])
+            for i, (j, c) in enumerate(shifts):
+                tk["pk"] = mm([tk["s"], tk["n2"]], P[3][:, j:192:3], T.pk[:, i], T.S[:, SL + 1 + c:SL + 1 + NA:4],
+                              i % 2 == 0, i % 2 == 1, mark=(i == 5))
+        elif kind == "S":
+            t = act([tk["s"]], T.sb[:], T.S[:, SL + 1:SL + 1 + NA])
+            tk["S"] = extract([t, tk["zk"]], P[4][:, 0:16], T.sb, 0, NA, ZK)
+        elif kind == "L":
+            tk["L"] = last[3] = cp([tk["pk"]], T.cel[:], P[3][:, 0:192])
+        elif kind == "K":
+            tk["K"] = ts([tk["S"]], T.kcu[:], P[4][:, 0:16], 0.5, ALU.subtract)
         elif kind == "k":
-            a_tt = act([v_kc, a_fill, l_tab], T.tt[:], T.TAB[:].indirect(T.kcu[:]), -1.0)
+            a_tt = act([tk["K"], tk["pad"], tk["tab0"], tk["tab1"]], T.tt[:], T.TAB[:].indirect(T.kcu[:]), -1.0, 1.0)
             a_tn = act([a_tt], T.tn[:], T.tt[:], BIG, 0.0, RELU)
-            mm([a_tt, a_zz], P[5][:, 0:NA], T.idb[:], T.tt[:], False, False, mark=False)
-            p_y = mm([a_tn], P[5][:, 0:NA], T.idb[:], T.tn[:], False, True)
+            mm([a_fill], P[5][:, 0:NA], T.m12[0:1, :], T.lo[0:1, 0:NA], True, False, mark=False)
+            mm([a_tt], P[5][:, 0:NA], T.idb[:], T.tt[:], False, False, mark=False)
+            tk["k"] = mm([a_tn], P[5][:, 0:NA], T.idb[:], T.tn[:], False, True)
         elif kind == "y":
-            v_yl = ts([p_y], T.yl[:], P[5][:, 0:NA], -1.0, ALU.mult, 0.0, ALU.max)
+            tk["y"] = ts([tk["k"]], T.yl[:], P[5][:, 0:NA], -1.0, ALU.mult, float(PAD), ALU.add)
+        elif kind == "x":
+            lo, hi = XC[k], XC[k + 1]
+            tx[k] = lin(q, [tk["xb"], tk["L"], a_fill] + upto(tw, UC, NV), T.XL[:, 16 * lo:16 * hi],
+                        T.X[:].indirect(T.cel[:, lo:hi]))
+        elif kind == "E":
+            c0, c1 = CC[k], CC[k + 1]
+            for bank, z in zip(BANKS[k], (ZA, ZV)):
+                tk["E", bank] = extract(upto(tx, XC, c1) + [last.get(bank), tk["n4"]], P[bank][:, 0:c1 - c0], T.XL,
+                                        16 * c0, 16 * c1, z)
+        elif kind in ("l", "r"):
+            c0, c1 = CC[k], CC[k + 1]
+            bank = BANKS[k][kind == "r"]
+            lst, done = (T.al, tl) if kind == "l" else (T.vl, tr_)
+            done[k] = ts([tk["E", bank]], lst[:, c0:c1], P[bank][:, 0:c1 - c0], C(5), ALU.subtract, float(TOP), ALU.min)
+        elif kind == "p":
+            lo, hi = AC[k], AC[k + 1]
+            tp[k] = lin(q, upto(tl, CC, hi) + [arrC, tk["ch"], tk["pad"]], T.CA[:, 16 * lo:16 * hi],
+                        T.CH[:].indirect(T.al[:, lo:hi]))
+        elif kind == "q":
+            lo, hi = VCUT[k], VCUT[k + 1]
+            tq[k] = tt(upto(tr_, CC, hi) + upto(tp, AC, hi), T.S[:, VO + PAD + 16 * lo:VO + PAD + 16 * hi],
+                       T.CH[:].indirect(T.vl[:, lo:hi]), T.CA[:, 16 * lo:16 * hi], ALU.add)
         else:
-            m0, m1 = YS[c]
-            n, t = [x for x in vc if x[0] >= 12 * m1][0]
-            w = T.VC[:, 0:PAD + n].indirect(T.yl[:, m0:m1])
+            m0, m1 = YC[k], YC[k + 1]
+            n = min(c for c in VCUT if 16 * c >= 12 * m1)
             o = T.Y[:, 16 * m0:16 * m1]
-            t = act([v_yl, t, a_fill], o, w) if YQ[c] == "A" else cp([v_yl, t, a_fill], o, w)
+            t = lin(q, upto(tq, VCUT, n) + [tk["y"], a_fill], o,
+                    T.S[:, VO:VO + PAD + 16 * n].indirect(T.yl[:, m0:m1]))
             dma("S", [t], [(T.y[:, 16 * m0:16 * m1], o)])
 
     wait("G", [(s, n) for s, n in cnt.items()])

@@ -6,26 +6,28 @@ ID = ActivationFunctionType.Identity
 RELU = ActivationFunctionType.Relu
 NV, NB, NA = 4096, 256, 256
 PAD = 16
-TOP = PAD + NV + 4 * NB
+MID, FO = PAD + NV, PAD + NV + 32
+TOP = FO + 4 * NB
 BIG = 8192.0
 SL, VO = 640, 904
 BH, BL, DF, SG, FAR, FS, MARK = 13, 14, 1, 15, 3, 2, 0
+SG_ON_G = True
 WA = 768
-UC = [0, 384, 1344, 2560, 4096]
+UC = [0, 1344, 2112, 3584, 4096]
 CC = [0, 64, 128, 192]
 BANKS = [(6, 7), (0, 1), (2, 3)]
-XC = [0, 32, 64, 114, 192]
-AC = [0, 32, 64, 96, 128, 192]
-VCUT = [0, 32, 64, 90, 128, 154, 176, 192]
-YC = [0, 40, 84, 130, 166, 204, 230, 256]
-ORDER = ("lt ld col ce n1 kd g3 TV g2 n3 en t g1 h3 g0 h2 u3A h1 n2 h0 tb u1A tab0 e tab1 pad w3 c MA xb u2A m s n4 v1A w2 "
-         "u0A z1 S L w0 x1V x0A x2V x3A E0 l0 K p0V k r0 q0 p1A E1 y q1 o0A l1 p2V p3A E2 r1 o1A q2 l2 q3 p4A r2 o3V "
-         "o2A q4 q5 o4A q6 o5V o6A").split()
+XC = [0, 32, 64, 100, 192]
+AC = [0, 26, 64, 90, 128, 192]
+VCUT = [0, 24, 64, 126, 154, 178, 192]
+YC = [0, 28, 84, 118, 168, 204, 228, 256]
+ORDER = ("ld tab0 ce en n0 kd pad TV g0 tab1 tab2 g1 cm h0 t g2 col h1 g3 h2 u0A n1 h3 u1V n3 e n2 c f w0 v2A xb n4 s u2A "
+         "w1 S u3A z2 tab3 MA w3 L x0V x1A m K x3A E0 x2V k l0 jV p0V p1A r0 E1 y q0 l1 o0A q1 p2A E2 p3V o1A r1 l2 "
+         "q2 p4A r2 o2V o3A q3 q4 o4A q5 o5V o6A").split()
 
 F, B, I, U, H = "float32", "bfloat16", "int32", "uint16", "float16"
 SCRATCH = {
     "W": ("sbuf", [128, NV], B), "X": ("sbuf", [128, NV + 4 * NB], B), "CH": ("sbuf", [128, TOP + 16], B),
-    "TAB": ("sbuf", [128, 16 + NV], B), "tbi": ("sbuf", [128, 512], I), "tbb": ("sbuf", [128, 512], B),
+    "TAB": ("sbuf", [128, 16 + NV], I), "oh": ("sbuf", [128, 128], F), "rt": ("sbuf", [128, 4], F),
     "GA": ("sbuf", [128, 2048], B), "GV": ("sbuf", [128, 2048], B), "sb": ("sbuf", [128, 256], B),
     "UE": ("sbuf", [128, NV], B), "XL": ("sbuf", [128, 3072], B), "CA": ("sbuf", [128, 3072], B),
     "S": ("sbuf", [128, VO + PAD + 3072], F), "Y": ("sbuf", [128, 4096], F),
@@ -38,7 +40,7 @@ SCRATCH = {
     "cei": ("sbuf", [128, 32, 12], I), "cep": ("sbuf", [128, 32, 16], F),
     "pi": ("sbuf", [128, 8], I), "col": ("sbuf", [128, 16], F),
     "lb": ("sbuf", [128, 8, 16], F), "lk": ("sbuf", [128, 512], B),
-    "idf": ("sbuf", [128, 128], F), "idb": ("sbuf", [128, 128], B), "zz": ("sbuf", [128, 736], B),
+    "idf": ("sbuf", [128, 128], F), "idb": ("sbuf", [128, 128], B), "zz": ("sbuf", [128, 752], B),
     "kdl": ("sbuf", [128, 512], B), "pk": ("sbuf", [128, 6, 8, 16], F),
     "dump": ("sbuf", [128, 32], F), "m12": ("sbuf", [128, 128], B),
     "ee": ("sbuf", [128, 512], B), "cum": ("sbuf", [128, 512], H),
@@ -173,10 +175,10 @@ def rank_program(g, core, T, topo):
     l_ce = [dma(q, [], [(T.cei[:, 4 * k:4 * k + 4, :], T.ce[k]) for k in range(k0, k0 + 4)])
             for q, k0 in (("A", 0), ("S", 4))]
     l_kd = dma("S", [], [(T.kdi[0:32, :], T.kd[:])])
+    l_en = dma("S", [], [(T.eni[:, 0:256], T.ea[:]), (T.eni[:, 256:512], T.eb[:])])
 
     g_hi = iota(T.col[:, 6:8], [[-PAD, 2]], 0, 256)
     g_lo = iota(T.lo[:], [[1, 288]], 0, 0)
-    g_p = iota(T.pi[:, 0:1], [[0, 1]], 0, 1, False)
     v_w = mset(T.W[:, 0:WA], 1.0)
     v_w2 = mset(T.W[:, WA:NV - WA], 1.0)
     act([v_w], T.W[:, NV - WA:], T.W[:, 0:WA])
@@ -185,8 +187,7 @@ def rank_program(g, core, T, topo):
     w_n = dma("S", [a_w, v_w2], [(T.W[BL::16, :], T.lo[:, 0:256]), (T.W[DF + 8::16, :], T.lo[:, 0:256]),
                                  (T.W[BH::16, :], T.hi[:]), (T.W[DF::16, :], T.hi[:])])
     w_s = dma("S", [v_s], [(T.W[SG::16, :], T.sc[:])])
-    l_en = dma("S", [], [(T.eni[:, 0:256], T.ea[:]), (T.eni[:, 256:512], T.eb[:])])
-    sl = PAD + NV + NB * rank
+    sl = FO + NB * rank
     Wt = [w_n, w_s]
     v_zz = mset(T.zz[:], 0.0)
     v_cb = cp([l_cb], T.cbu[:], T.cbi[:])
@@ -209,7 +210,7 @@ def rank_program(g, core, T, topo):
     act([], T.m12[0:1, :], T.lo[0:1, 0:128], 0.0, -12.0)
     act([g_id], T.idb[:], T.idf[:])
     a_fill = fill(T.S[:, SL:VO + PAD], VO + PAD - SL, 0.0)
-    ZP, ZQ, ZK, ZA, ZV, ZERO = 0, 144, 288, 432, 576, T.zz[:, 720:736]
+    ZP, ZQ, ZK, ZA, ZV = 0, 144, 288, 432, 576
     Z = lambda z: T.zz[:, z + 15:z + 144:16]
     shifts = [(0, 0), (0, 1), (1, 1), (1, 2), (2, 2), (2, 3)]
 
@@ -251,42 +252,43 @@ def rank_program(g, core, T, topo):
                 end = step == into0[-1] and v == 3
                 tk["case"] = mm([t, g_kd], P[0][:, 128 * v:128 * v + 128], T.kdl[0:32, 128 * v:128 * v + 128],
                                 T.kdb[0:32, :], step == into0[0] and v == 0, end, mark=end)
+        elif kind == "cm":
+            mm([tk["n0"]], P[1][:, 0:4], T.oh[0:16, :], T.rt[0:16, :], True, False, mark=False)
+            tk["cm"] = mm([], P[1][:, 3:4], T.idf[:], C(7), False, True)
         elif kind == "col":
-            r = T.pi[:, 1:2]
-            t = ts([g_p], r, T.pi[:, 0:1], 15, ALU.bitwise_and)
-            t1 = ts([t], C(1), r, float(BH), ALU.is_ge, 1.0, ALU.subtract)
-            ts([t], C(3), r, float(MARK), ALU.not_equal)
-            ts([t], C(4), r, 11.0, ALU.is_equal)
-            ts([t, g_hi], C(5), r, -256.0, ALU.mult, C(7), ALU.add)
-            tk["col"] = ts([t1], C(2), r, float(SG), ALU.is_ge, C(1), ALU.add)
+            tk["col"] = last[1] = cp([tk["cm"]], T.col[:, 2:6], P[1][:, 0:4])
+        elif kind == "n" and k == 0:
+            t = iota(T.rt[0:16, 0:3], [[1, 3]], -1, 0)
+            iota(T.rt[0:16, 3:4], [[0, 1]], 0, -256)
+            t = put([t], T.rt[0:16, 0:1], T.rt[0:16, 0:1], [[0, 1]], -SG, 1.0)
+            put([g_kd], T.oh[0:16, :], T.zz[0:16, 0:128], [[0, 8], [-1, 16]], 0, 1.0)
+            t = put([t], T.rt[0:16, 0:3:2], T.rt[0:16, 0:3:2], [[BH - MARK, 2]], -BH, 0.0)
+            tk["n0"] = put([t], T.rt[0:16, 0:1], T.rt[0:16, 0:1], [[0, 1]], -BL, 0.0)
         elif kind == "en":
             tk[kind] = cp([l_en], T.enu[:], T.eni[:])
-        elif kind == "tb":
-            tk[kind] = ts([tk["lt"]], T.tbb[:], T.tbi[:], 1.0, ALU.add)
         elif kind == "tab":
-            tk[step] = dma("S", [tk["tb"]],
-                           [(T.TAB[16 * j:16 * j + 16, 16:16 + NV], T.tbb[:]) for j in range(4 * k, 4 * k + 4)])
+            tk[step] = dma("S", [], [(T.TAB[16 * j:16 * j + 16, 16:16 + NV], T.tab[:]) for j in (2 * k, 2 * k + 1)])
         elif kind == "n" and k == 1:
-            t = coef([g_kd], Z(ZQ), 11, 1.0)
-            t1 = coef([], Z(ZP), 11, float(SL))
+            t = t1 = coef([tk["n0"]], Z(ZP), 11, SL - 2048.0)
             for row in (12, 13):
-                t = coef([t], Z(ZQ), row, -1.0)
-                t1 = coef([t1], Z(ZP), row, -2048.0)
+                t = coef([t], Z(ZQ), row, 0.25)
+                t1 = coef([t1], Z(ZP), row, 1024.0)
             tk["n1"] = iota(T.dump[:], [[16, 32]], 0, 1)
         elif kind == "n" and k == 2:
-            t = iota(T.pk[:], [[0, 768]], 0, 0)
+            t = tk["pad"]
             for i, (j, c) in enumerate(shifts):
                 sh = 12 * c - 16 * j
                 r0, r1 = max(0, sh), min(16, 12 + sh)
                 tk["n2"] = put([t], T.pk[:, i, :, r0:r1], T.pk[:, i, :, r0:r1], [[-16, 8], [-1, r1 - r0]], sh - r0, 1.0)
         elif kind == "n" and k == 3:
             t = coef([g_kd], Z(ZK), 14, 1.0)
+            iota(T.TAB[:, 0:16], [[0, 16]], -1, 0, False)
             tk["zk"] = coef([t], Z(ZK), 15, 1.0)
         elif kind == "n":
             zb, t = T.zz[:, ZA + 15:720:16], g_kd
             for row, val in ((BH, 1.0), (BL, 1.0), (SG, BIG), (FS, BIG)):
                 t = put([t], zb, zb, [[0, 2], [-16, 9]], -row, val)
-            for row, val in ((DF, -1.0), (DF + 8, -1.0), (FAR, 1.0), (FAR + 8, 1.0), (MARK, float(NV))):
+            for row, val in ((DF, -1.0), (DF + 8, -1.0), (FAR, 1.0), (FAR + 8, 1.0), (MARK, float(FO - PAD))):
                 tk["n4"] = t = coef([t], Z(ZA), row, val)
         elif kind == "u":
             lo, hi = UC[k], UC[k + 1]
@@ -294,7 +296,7 @@ def rank_program(g, core, T, topo):
                         1.0 if "z%d" % k in ORDER else C(2))
         elif kind == "v":
             lo, hi = UC[k], UC[k + 1]
-            tk["v", k] = lin(q, Wt + [tk["en"], tk["col"]], T.X[:, lo:hi], gw(T.enu, NV + lo, NV + hi), C(3))
+            tk["v", k] = lin(q, Wt + [tk["en"], tk["col"]], T.X[:, lo:hi], gw(T.enu, NV + lo, NV + hi), C(4))
         elif kind == "z":
             lo, hi = UC[k], UC[k + 1]
             tw[k] = dma("S", [tk["v", k], tu[k]], [(T.X[FAR::8, lo:hi], T.UE[DF::8, lo:hi]),
@@ -304,10 +306,10 @@ def rank_program(g, core, T, topo):
             tw[k] = tt([tu[k]], T.X[:, lo:hi], gw(T.enu, NV + lo, NV + hi), T.UE[:, lo:hi], ALU.add)
         elif kind == "ld":
             tk["ch"] = dma("S", [], [(T.CH[:, PAD:PAD + NV], T.ch[:]), (T.CH[:, sl:sl + NB], T.ch[:, 0:NB])])
-        elif kind == "lt":
-            tk["lt"] = dma("S", [], [(T.tbi[:], T.tab[:])])
         elif kind == "pad":
-            tk["pad"] = dma("S", [v_zz], [(T.CH[:, 0:PAD], ZERO), (T.CH[:, TOP:], ZERO), (T.TAB[:, 0:16], ZERO)])
+            tk["pad"] = dma("S", [v_zz, a_fill], [(T.CH[:, a:a + n], T.zz[:, 720:720 + n])
+                                                  for a, n in ((0, PAD), (MID, FO - MID), (TOP, 16))] +
+                            [(T.pk[:, j:j + 2], T.S[:, SL:SL + 256]) for j in (0, 2, 4)])
         elif kind == "T":
             for a, b in blocks:
                 tk["T"] = lin(q, Wt + [v_cb], T.X[:, NV + NB * a:NV + NB * b], gw(T.cbu, NV + NB * a, NV + NB * b))
@@ -322,34 +324,43 @@ def rank_program(g, core, T, topo):
                 tk["M"] = lin(q, [tk["ch"], v_cb], T.MC[:, NB * a:NB * b],
                               T.CH[:, PAD:PAD + NV].indirect(T.cbu[:, 256 + 16 * a:256 + 16 * b]))
         elif kind == "m":
-            sentC, arrC = send([tk["M"]], T.MC, T.CH, 0, PAD + NV, "arrC", "sentC")
+            sentC, arrC = send([tk["M"]], T.MC, T.CH, 0, FO, "arrC", "sentC")
         elif kind == "e":
-            tk["e"] = t = ts([tk["case"], tk["col"]], T.ee[:], P[0][:], -127.5, ALU.is_equal, C(4), ALU.max)
-            v_sc = op("V", [t], lambda e: e.tensor_tensor_scan(T.cum[:], T.ee[:], T.ee[:], 0.0, ALU.add, ALU.max))
-            extract([t, tk["n1"]], P[2][:, 0:32], T.ee, 0, 512, ZP, True, False)
+            tk["e"] = act([tk["case"]], T.ee[:], P[0][:], 1.0, 127.0, ActivationFunctionType.Sign)
+            extract([tk["e"], tk["n1"]], P[2][:, 0:32], T.ee, 0, 512, ZP, True, False)
+        elif kind == "f":
+            v_sc = op("V", [tk["e"]], lambda e: e.tensor_tensor_scan(T.cum[:], T.ee[:], T.ee[:], 0.0, ALU.add, ALU.add))
             tk["q"] = extract([v_sc], P[2][:, 0:32], T.cum, 0, 512, ZQ, False, True)
         elif kind == "c":
-            tk["c"] = last[0] = act([tk["e"]], T.cev[:], P[0][:])
+            tk["c"] = last[0] = act([tk["case"]], T.cev[:], P[0][:])
         elif kind == "s":
             t = tt([tk["q"]], T.tf[:], P[2][:, 0:32], T.dump[:], ALU.max)
             last[2] = t = cp([t], T.tu[:], T.tf[:])
-            tk["s"] = cp([t, tk["c"], a_fill], T.S[:, 0:VO].indirect(T.tu[:]), T.cev[:])
+            tk["s"] = cp([t, tk["c"], tk["pad"]], T.S[:, 0:VO].indirect(T.tu[:]), T.cev[:])
             for i, (j, c) in enumerate(shifts):
                 tk["pk"] = mm([tk["s"], tk["n2"]], P[3][:, j:192:3], T.pk[:, i], T.S[:, SL + 1 + c:SL + 1 + NA:4],
                               i % 2 == 0, i % 2 == 1, mark=(i == 5))
         elif kind == "S":
-            t = act([tk["s"]], T.sb[:], T.S[:, SL + 1:SL + 1 + NA])
+            if SG_ON_G:
+                t = put([tk["s"]], T.sb[:], T.S[:, SL + 1:SL + 1 + NA], [[0, NA]], 1, 0.0)
+            else:
+                t = act([tk["s"]], T.sb[:], T.S[:, SL + 1:SL + 1 + NA])
             tk["S"] = extract([t, tk["zk"]], P[4][:, 0:16], T.sb, 0, NA, ZK)
+            mm([a_fill], P[5][:, 0:NA], T.m12[0:1, :], T.lo[0:1, 0:NA], True, False, mark=False)
         elif kind == "L":
             tk["L"] = last[3] = cp([tk["pk"]], T.cel[:], P[3][:, 0:192])
         elif kind == "K":
             tk["K"] = ts([tk["S"]], T.kcu[:], P[4][:, 0:16], 0.5, ALU.subtract)
         elif kind == "k":
-            a_tt = act([tk["K"], tk["pad"], tk["tab0"], tk["tab1"]], T.tt[:], T.TAB[:].indirect(T.kcu[:]), -1.0, 1.0)
-            a_tn = act([a_tt], T.tn[:], T.tt[:], BIG, 0.0, RELU)
-            mm([a_fill], P[5][:, 0:NA], T.m12[0:1, :], T.lo[0:1, 0:NA], True, False, mark=False)
-            mm([a_tt], P[5][:, 0:NA], T.idb[:], T.tt[:], False, False, mark=False)
-            tk["k"] = mm([a_tn], P[5][:, 0:NA], T.idb[:], T.tn[:], False, True)
+            tk["tt"] = ts([tk["K"], tk["zk"]] + [tk["tab%d" % j] for j in range(4)], T.tt[:],
+                          T.TAB[:].indirect(T.kcu[:]), -1.0, ALU.mult)
+        elif kind == "j":
+            if q == "A":
+                t = act([tk["tt"]], T.tn[:], T.tt[:], BIG, 0.0, RELU)
+            else:
+                t = ts([tk["tt"]], T.tn[:], T.tt[:], BIG, ALU.mult, 0.0, ALU.max)
+            mm([tk["tt"]], P[5][:, 0:NA], T.idb[:], T.tt[:], False, False, mark=False)
+            tk["k"] = mm([t], P[5][:, 0:NA], T.idb[:], T.tn[:], False, True)
         elif kind == "y":
             tk["y"] = ts([tk["k"]], T.yl[:], P[5][:, 0:NA], -1.0, ALU.mult, float(PAD), ALU.add)
         elif kind == "x":
@@ -358,21 +369,22 @@ def rank_program(g, core, T, topo):
                         T.X[:].indirect(T.cel[:, lo:hi]))
         elif kind == "E":
             c0, c1 = CC[k], CC[k + 1]
-            for bank, z in zip(BANKS[k], (ZA, ZV)):
+            for bank, z in zip(BANKS[k], (ZV, ZA)):
                 tk["E", bank] = extract(upto(tx, XC, c1) + [last.get(bank), tk["n4"]], P[bank][:, 0:c1 - c0], T.XL,
                                         16 * c0, 16 * c1, z)
         elif kind in ("l", "r"):
             c0, c1 = CC[k], CC[k + 1]
             bank = BANKS[k][kind == "r"]
             lst, done = (T.al, tl) if kind == "l" else (T.vl, tr_)
-            done[k] = ts([tk["E", bank]], lst[:, c0:c1], P[bank][:, 0:c1 - c0], C(5), ALU.subtract, float(TOP), ALU.min)
+            done[k] = ts([tk["E", bank]], lst[:, c0:c1], P[bank][:, 0:c1 - c0], C(5), ALU.subtract,
+                         float(MID if kind == "l" else TOP), ALU.min)
         elif kind == "p":
             lo, hi = AC[k], AC[k + 1]
-            tp[k] = lin(q, upto(tl, CC, hi) + [arrC, tk["ch"], tk["pad"]], T.CA[:, 16 * lo:16 * hi],
-                        T.CH[:].indirect(T.al[:, lo:hi]))
+            tp[k] = lin(q, upto(tl, CC, hi) + [tk["ch"], tk["pad"]], T.CA[:, 16 * lo:16 * hi],
+                        T.CH[:, 0:FO].indirect(T.al[:, lo:hi]))
         elif kind == "q":
             lo, hi = VCUT[k], VCUT[k + 1]
-            tq[k] = tt(upto(tr_, CC, hi) + upto(tp, AC, hi), T.S[:, VO + PAD + 16 * lo:VO + PAD + 16 * hi],
+            tq[k] = tt(upto(tr_, CC, hi) + upto(tp, AC, hi) + [arrC], T.S[:, VO + PAD + 16 * lo:VO + PAD + 16 * hi],
                        T.CH[:].indirect(T.vl[:, lo:hi]), T.CA[:, 16 * lo:16 * hi], ALU.add)
         else:
             m0, m1 = YC[k], YC[k + 1]

from concourse.bass import DstId, RemoteDMATransfer
from concourse.mybir import AluOpType, ActivationFunctionType

ALU = AluOpType
ID = ActivationFunctionType.Identity
RELU = ActivationFunctionType.Relu
NV, NB, NA = 4096, 256, 256
PAD = 16
MID, FO = PAD + NV, PAD + NV + 32
TOP = FO + 4 * NB
BIG = 8192.0
SL, VO = 640, 904
BH, BL, DF, SG, FAR, FS, MARK = 13, 14, 1, 15, 3, 2, 0
SG_ON_G = True
WA = 768
UC = [0, 1344, 2112, 3584, 4096]
CC = [0, 64, 128, 192]
BANKS = [(6, 7), (0, 1), (2, 3)]
XC = [0, 32, 64, 100, 192]
AC = [0, 26, 64, 90, 128, 192]
VCUT = [0, 24, 64, 126, 154, 178, 192]
YC = [0, 28, 84, 118, 168, 204, 228, 256]
ORDER = ("ld tab0 ce en n0 kd pad TV g0 tab1 tab2 g1 cm h0 t g2 col h1 g3 h2 u0A n1 h3 u1V n3 e n2 c f w0 v2A xb n4 s u2A "
         "w1 S u3A z2 tab3 MA w3 L x0V x1A m K x3A E0 x2V k l0 jV p0V p1A r0 E1 y q0 l1 o0A q1 p2A E2 p3V o1A r1 l2 "
         "q2 p4A r2 o2V o3A q3 q4 o4A q5 o5V o6A").split()

F, B, I, U, H = "float32", "bfloat16", "int32", "uint16", "float16"
SCRATCH = {
    "W": ("sbuf", [128, NV], B), "X": ("sbuf", [128, NV + 4 * NB], B), "CH": ("sbuf", [128, TOP + 16], B),
    "TAB": ("sbuf", [128, 16 + NV], I), "oh": ("sbuf", [128, 128], F), "rt": ("sbuf", [128, 4], F),
    "GA": ("sbuf", [128, 2048], B), "GV": ("sbuf", [128, 2048], B), "sb": ("sbuf", [128, 256], B),
    "UE": ("sbuf", [128, NV], B), "XL": ("sbuf", [128, 3072], B), "CA": ("sbuf", [128, 3072], B),
    "S": ("sbuf", [128, VO + PAD + 3072], F), "Y": ("sbuf", [128, 4096], F),
    "MS": ("sbuf", [128, 4 * NB], B), "MC": ("sbuf", [128, 4 * NB], B),
    "lvc": ("sbuf", [128, 256], B), "sc": ("sbuf", [128, 256], B),
    "lo": ("sbuf", [128, 288], B), "hi": ("sbuf", [128, 256], B),
    "cbi": ("sbuf", [128, 320], I), "cbu": ("sbuf", [128, 320], U),
    "eni": ("sbuf", [128, 512], I), "enu": ("sbuf", [128, 512], U),
    "kdi": ("sbuf", [128, 128], I), "kdb": ("sbuf", [128, 128], B),
    "cei": ("sbuf", [128, 32, 12], I), "cep": ("sbuf", [128, 32, 16], F),
    "pi": ("sbuf", [128, 8], I), "col": ("sbuf", [128, 16], F),
    "lb": ("sbuf", [128, 8, 16], F), "lk": ("sbuf", [128, 512], B),
    "idf": ("sbuf", [128, 128], F), "idb": ("sbuf", [128, 128], B), "zz": ("sbuf", [128, 752], B),
    "kdl": ("sbuf", [128, 512], B), "pk": ("sbuf", [128, 6, 8, 16], F),
    "dump": ("sbuf", [128, 32], F), "m12": ("sbuf", [128, 128], B),
    "ee": ("sbuf", [128, 512], B), "cum": ("sbuf", [128, 512], H),
    "tf": ("sbuf", [128, 32], F), "tu": ("sbuf", [128, 32], U), "cev": ("sbuf", [128, 512], F),
    "cel": ("sbuf", [128, 192], U), "kcu": ("sbuf", [128, 16], U),
    "tt": ("sbuf", [128, 256], B), "tn": ("sbuf", [128, 256], B), "yl": ("sbuf", [128, 256], U),
    "al": ("sbuf", [128, 192], U), "vl": ("sbuf", [128, 192], U),
}
for _k in range(8):
    SCRATCH["P%d" % _k] = ("psum", [128, 512], F)
SEMAPHORES = ["sV", "sA", "sP", "sG", "arrS", "arrC", "sentS", "sentC"] + ["d%d" % k for k in range(40)]


def engine_sets(topo, src, dsts):
    sets, used = {}, set()
    order = sorted(dsts, key=lambda d: len(topo.engines(src, d)))
    for k, d in enumerate(order):
        mine = topo.engines(src, d)
        left = [e for e in mine if e not in used]
        rivals = len([p for p in order[k:] if topo.engines(src, p) == mine])
        n = 1
        while 2 * n * rivals <= len(left):
            n *= 2
        used.update(left[:n])
        sets[d] = left[:n]
    return sets


def rank_program(g, core, T, topo):
    rank = T.rank_of(core)
    if rank is None:
        return
    N = len(T.cores)
    peers = [q for q in range(N) if q != rank]
    Q = {"V": g.vector, "A": g.scalar, "P": g.tensor, "G": g, "S": g.sync}
    cnt = {}
    seen = {}
    nd = [0]

    def wait(q, deps):
        need = {}
        for d in deps:
            if d is not None:
                need[d[0]] = max(need.get(d[0], 0), d[1])
        for s, n in need.items():
            if seen.get((q, s), 0) < n:
                Q[q].wait_ge(T.sem[s], n)
                seen[(q, s)] = n

    def op(q, deps, fn, mark=True):
        wait(q, deps)
        ins = fn(Q[q])
        if not mark:
            return None
        s = "s" + q
        cnt[s] = cnt.get(s, 0) + 1
        ins.then_inc(T.sem[s], 1)
        return (s, cnt[s])

    def dma(q, deps, pairs):
        wait(q, deps)
        s = "d%d" % nd[0]
        nd[0] += 1
        for o, i in pairs:
            Q[q].dma_start(o, i).then_inc(T.sem[s], 16)
        cnt[s] = 16 * len(pairs)
        return (s, cnt[s])

    def ts(deps, o, i, s1, op0, s2=None, op1=None):
        if op1 is None:
            return op("V", deps, lambda e: e.tensor_scalar(o, i, s1, None, op0))
        return op("V", deps, lambda e: e.tensor_scalar(o, i, s1, s2, op0, op1))

    def cp(deps, o, i):
        return op("V", deps, lambda e: e.tensor_copy(o, i))

    def tt(deps, o, a, b, alu):
        return op("V", deps, lambda e: e.tensor_tensor(o, a, b, alu))

    def mset(o, val):
        return op("V", [], lambda e: e.memset(o, val))

    def act(deps, o, i, scale=1.0, bias=0.0, func=ID):
        return op("A", deps, lambda e: e.activation(o, i, func, bias=bias, scale=scale))

    def lin(q, deps, o, i, scale=1.0):
        return act(deps, o, i, scale) if q == "A" else ts(deps, o, i, scale, ALU.mult)

    def mm(deps, o, l, r, start, stop, mark=True):
        return op("P", deps, lambda e: e.matmul(o, l, r, start, stop), mark)

    def put(deps, o, i, pat, base, val):
        return op("G", deps, lambda e: e.affine_select(o, i, pat, ALU.not_equal, val, base, 1))

    def iota(o, pat, base, cm, fl=True):
        if fl:
            return op("G", [], lambda e: e.iota(o, pat, base, cm, allow_small_or_imprecise_dtypes=True))
        return op("G", [], lambda e: e.iota(o, pat, base, cm))

    def extract(deps, o, src, lo, hi, z0, start=True, stop=True):
        t = None
        for u in range(16):
            t = mm(deps, o, T.zz[:, z0 + 15 - u:z0 + 143 - u], src[:, lo + u:hi:16], start and u == 0,
                   stop and u == 15, mark=(stop and u == 15))
        return t

    others = [T.cores[q] for q in peers]
    eng = engine_sets(topo, core, others)
    n_out = sum(len(v) for v in eng.values())
    n_in = sum(len(engine_sets(topo, c, [d for d in T.cores if d != c])[core]) for c in others)

    def send(deps, src, dst, lo_src, lo_dst, arr, sent):
        wait("G", deps)
        tr = []
        for q in peers:
            rid, pid, _ = topo.addr(T.cores[q])
            a, b = lo_src + NB * q, lo_dst + NB * rank
            tr.append(RemoteDMATransfer(dst_ids=[DstId(rid=rid, pnc=pid)],
                                        dma_engine_mask=sum(1 << e for e in eng[T.cores[q]]),
                                        remote_sem=T.sem[arr], src=src[:, a:a + NB], dst=dst[:, b:b + NB]))
        g.remote_dma_fused(tr, local_sem=T.sem[sent])
        cnt[sent], cnt[arr] = n_out, n_in
        return (sent, n_out), (arr, n_in)

    C = lambda k: T.col[:, k:k + 1]
    P = [T["P%d" % k] for k in range(8)]
    blocks = [b for b in [(0, rank), (rank + 1, N)] if b[1] > b[0]]
    step = ""

    l_lv = dma("S", [], [(T.lvc[:], T.lv[:])])
    l_cb = dma("S", [], [(T.cbi[:, 0:256], T.cor[:]), (T.cbi[:, 256:320], T.bl[:])])
    l_ce = [dma(q, [], [(T.cei[:, 4 * k:4 * k + 4, :], T.ce[k]) for k in range(k0, k0 + 4)])
            for q, k0 in (("A", 0), ("S", 4))]
    l_kd = dma("S", [], [(T.kdi[0:32, :], T.kd[:])])
    l_en = dma("S", [], [(T.eni[:, 0:256], T.ea[:]), (T.eni[:, 256:512], T.eb[:])])

    g_hi = iota(T.col[:, 6:8], [[-PAD, 2]], 0, 256)
    g_lo = iota(T.lo[:], [[1, 288]], 0, 0)
    v_w = mset(T.W[:, 0:WA], 1.0)
    v_w2 = mset(T.W[:, WA:NV - WA], 1.0)
    act([v_w], T.W[:, NV - WA:], T.W[:, 0:WA])
    a_w = act([g_lo], T.hi[:], T.lo[:, 0:256], 0.0, C(6))
    v_s = ts([l_lv], T.sc[:], T.lvc[:], 0.0, ALU.is_lt, 0.5, ALU.subtract)
    w_n = dma("S", [a_w, v_w2], [(T.W[BL::16, :], T.lo[:, 0:256]), (T.W[DF + 8::16, :], T.lo[:, 0:256]),
                                 (T.W[BH::16, :], T.hi[:]), (T.W[DF::16, :], T.hi[:])])
    w_s = dma("S", [v_s], [(T.W[SG::16, :], T.sc[:])])
    sl = FO + NB * rank
    Wt = [w_n, w_s]
    v_zz = mset(T.zz[:], 0.0)
    v_cb = cp([l_cb], T.cbu[:], T.cbi[:])

    def fill(o, n, val):
        return act([g_lo], o, T.lo[:, 0:n], 0.0, val)

    def coef(deps, ap, row, val):
        return put(deps, ap, ap, [[-16, 9]], -row, val)

    t = iota(T.lb[:], [[0, 128]], 0, 0)
    g_id = put([t], T.idf[:], T.lb[:], [[-1, 128]], 0, 1.0)
    put([g_id], T.lb[:, :, 12:16:2], T.lb[:, :, 12:16:2], [[-16, 8], [0, 2]], -SG, 1.0)
    g_lb = put([], T.lb[:, :, 13], T.lb[:, :, 13], [[-16, 8]], -SG, -1.0)
    g_kd = put([v_zz], T.kdl[0:32, :], T.zz[0:32, 0:512], [[-1, 4], [-4, 8], [1000, 16]], -15000, 1.0)
    a_cz = fill(T.cep[:, :, 12:16], 128, 0.0)
    for k in range(4):
        a_l = act([g_lb], T.lk[:, 128 * k:128 * k + 128], T.lb[:], float(16 << k))
    fill(T.X[:, NV + NB * rank:NV + NB * rank + NB], NB, -1.0)
    act([], T.m12[0:1, :], T.lo[0:1, 0:128], 0.0, -12.0)
    act([g_id], T.idb[:], T.idf[:])
    a_fill = fill(T.S[:, SL:VO + PAD], VO + PAD - SL, 0.0)
    ZP, ZQ, ZK, ZA, ZV = 0, 144, 288, 432, 576
    Z = lambda z: T.zz[:, z + 15:z + 144:16]
    shifts = [(0, 0), (0, 1), (1, 1), (1, 2), (2, 2), (2, 3)]

    def gw(lst, lo, hi):
        return T.W[:].indirect(lst[:, lo // 16:hi // 16])

    def upto(done, cuts, hi):
        return [done[k] for k in range(len(cuts) - 1) if cuts[k] < hi]

    into0 = [s for s in ORDER if s[0] in "hab" or s in ("ce", "kd")]
    tk, tu, tw, tx, tp, tq, tl, tr_ = {}, {}, {}, {}, {}, {}, {}, {}
    last = {}
    for step in ORDER:
        q = step[-1]
        name = step[:-1] if len(step) > 1 and q in "AV" else step
        kind, k = (name[:-1], int(name[-1])) if name[-1].isdigit() else (name, 0)
        s = slice(512 * k, 512 * k + 512)
        if kind == "g":
            tk[step] = act(Wt + [v_cb], T.GA[:, s], gw(T.cbu, 512 * k, 512 * k + 512), 0.0625)
        elif kind in ("h", "a", "b"):
            low, high = gw(T.cbu, 512 * k, 512 * k + 512), gw(T.cbu, 2048 + 512 * k, 2560 + 512 * k)
            if kind == "h":
                t = tt(Wt + [tk["g%d" % k]], T.GV[:, s], high, T.GA[:, s], ALU.add)
            elif kind == "a":
                t = lin(q, Wt + [v_cb], T.GA[:, s], low, 0.0625)
            else:
                t = lin(q, Wt + [v_cb], T.GV[:, s], high)
            tk["case"] = mm([t, a_l], P[0][:], T.lk[:, 128 * k:128 * k + 128], (T.GA if kind == "a" else T.GV)[:, s],
                            step == into0[0], step == into0[-1], mark=step == into0[-1])
        elif kind == "ce":
            for c in range(4):
                t = cp(l_ce + [a_cz], T.cep[:, 8 * c:8 * c + 8, 0:12], T.cei[:, c::4, :])
                end = step == into0[-1] and c == 3
                tk["case"] = mm([t, g_id], P[0][:, c::4], T.cep[:, 8 * c:8 * c + 8, :], T.idf[:],
                                step == into0[0] and c == 0, end, mark=end)
        elif kind == "kd":
            t = ts([l_kd], T.kdb[0:32, :], T.kdi[0:32, :], 256.0, ALU.mult, 144.0, ALU.add)
            for v in range(4):
                end = step == into0[-1] and v == 3
                tk["case"] = mm([t, g_kd], P[0][:, 128 * v:128 * v + 128], T.kdl[0:32, 128 * v:128 * v + 128],
                                T.kdb[0:32, :], step == into0[0] and v == 0, end, mark=end)
        elif kind == "cm":
            mm([tk["n0"]], P[1][:, 0:4], T.oh[0:16, :], T.rt[0:16, :], True, False, mark=False)
            tk["cm"] = mm([], P[1][:, 3:4], T.idf[:], C(7), False, True)
        elif kind == "col":
            tk["col"] = last[1] = cp([tk["cm"]], T.col[:, 2:6], P[1][:, 0:4])
        elif kind == "n" and k == 0:
            t = iota(T.rt[0:16, 0:3], [[1, 3]], -1, 0)
            iota(T.rt[0:16, 3:4], [[0, 1]], 0, -256)
            t = put([t], T.rt[0:16, 0:1], T.rt[0:16, 0:1], [[0, 1]], -SG, 1.0)
            put([g_kd], T.oh[0:16, :], T.zz[0:16, 0:128], [[0, 8], [-1, 16]], 0, 1.0)
            t = put([t], T.rt[0:16, 0:3:2], T.rt[0:16, 0:3:2], [[BH - MARK, 2]], -BH, 0.0)
            tk["n0"] = put([t], T.rt[0:16, 0:1], T.rt[0:16, 0:1], [[0, 1]], -BL, 0.0)
        elif kind == "en":
            tk[kind] = cp([l_en], T.enu[:], T.eni[:])
        elif kind == "tab":
            tk[step] = dma("S", [], [(T.TAB[16 * j:16 * j + 16, 16:16 + NV], T.tab[:]) for j in (2 * k, 2 * k + 1)])
        elif kind == "n" and k == 1:
            t = t1 = coef([tk["n0"]], Z(ZP), 11, SL - 2048.0)
            for row in (12, 13):
                t = coef([t], Z(ZQ), row, 0.25)
                t1 = coef([t1], Z(ZP), row, 1024.0)
            tk["n1"] = iota(T.dump[:], [[16, 32]], 0, 1)
        elif kind == "n" and k == 2:
            t = tk["pad"]
            for i, (j, c) in enumerate(shifts):
                sh = 12 * c - 16 * j
                r0, r1 = max(0, sh), min(16, 12 + sh)
                tk["n2"] = put([t], T.pk[:, i, :, r0:r1], T.pk[:, i, :, r0:r1], [[-16, 8], [-1, r1 - r0]], sh - r0, 1.0)
        elif kind == "n" and k == 3:
            t = coef([g_kd], Z(ZK), 14, 1.0)
            iota(T.TAB[:, 0:16], [[0, 16]], -1, 0, False)
            tk["zk"] = coef([t], Z(ZK), 15, 1.0)
        elif kind == "n":
            zb, t = T.zz[:, ZA + 15:720:16], g_kd
            for row, val in ((BH, 1.0), (BL, 1.0), (SG, BIG), (FS, BIG)):
                t = put([t], zb, zb, [[0, 2], [-16, 9]], -row, val)
            for row, val in ((DF, -1.0), (DF + 8, -1.0), (FAR, 1.0), (FAR + 8, 1.0), (MARK, float(FO - PAD))):
                tk["n4"] = t = coef([t], Z(ZA), row, val)
        elif kind == "u":
            lo, hi = UC[k], UC[k + 1]
            tu[k] = lin(q, Wt + [tk["en"], tk["col"]], T.UE[:, lo:hi], gw(T.enu, lo, hi),
                        1.0 if "z%d" % k in ORDER else C(2))
        elif kind == "v":
            lo, hi = UC[k], UC[k + 1]
            tk["v", k] = lin(q, Wt + [tk["en"], tk["col"]], T.X[:, lo:hi], gw(T.enu, NV + lo, NV + hi), C(4))
        elif kind == "z":
            lo, hi = UC[k], UC[k + 1]
            tw[k] = dma("S", [tk["v", k], tu[k]], [(T.X[FAR::8, lo:hi], T.UE[DF::8, lo:hi]),
                                                   (T.X[FS::16, lo:hi], T.UE[SG::16, lo:hi])])
        elif kind == "w":
            lo, hi = UC[k], UC[k + 1]
            tw[k] = tt([tu[k]], T.X[:, lo:hi], gw(T.enu, NV + lo, NV + hi), T.UE[:, lo:hi], ALU.add)
        elif kind == "ld":
            tk["ch"] = dma("S", [], [(T.CH[:, PAD:PAD + NV], T.ch[:]), (T.CH[:, sl:sl + NB], T.ch[:, 0:NB])])
        elif kind == "pad":
            tk["pad"] = dma("S", [v_zz, a_fill], [(T.CH[:, a:a + n], T.zz[:, 720:720 + n])
                                                  for a, n in ((0, PAD), (MID, FO - MID), (TOP, 16))] +
                            [(T.pk[:, j:j + 2], T.S[:, SL:SL + 256]) for j in (0, 2, 4)])
        elif kind == "T":
            for a, b in blocks:
                tk["T"] = lin(q, Wt + [v_cb], T.X[:, NV + NB * a:NV + NB * b], gw(T.cbu, NV + NB * a, NV + NB * b))
        elif kind == "t":
            sentS, arrS = send([tk["T"]], T.X, T.MS, NV, 0, "arrS", "sentS")
        elif kind == "xb":
            tk["xb"] = dma("S", [sentS, arrS, a_fill] + Wt,
                           [(T.X[FS::16, NV + NB * a:NV + NB * b], T.MS[SG::16, NB * a:NB * b]) for a, b in blocks] +
                           [(T.X[FAR::8, NV:], T.W[DF::8, 0:N * NB])])
        elif kind == "M":
            for a, b in blocks:
                tk["M"] = lin(q, [tk["ch"], v_cb], T.MC[:, NB * a:NB * b],
                              T.CH[:, PAD:PAD + NV].indirect(T.cbu[:, 256 + 16 * a:256 + 16 * b]))
        elif kind == "m":
            sentC, arrC = send([tk["M"]], T.MC, T.CH, 0, FO, "arrC", "sentC")
        elif kind == "e":
            tk["e"] = act([tk["case"]], T.ee[:], P[0][:], 1.0, 127.0, ActivationFunctionType.Sign)
            extract([tk["e"], tk["n1"]], P[2][:, 0:32], T.ee, 0, 512, ZP, True, False)
        elif kind == "f":
            v_sc = op("V", [tk["e"]], lambda e: e.tensor_tensor_scan(T.cum[:], T.ee[:], T.ee[:], 0.0, ALU.add, ALU.add))
            tk["q"] = extract([v_sc], P[2][:, 0:32], T.cum, 0, 512, ZQ, False, True)
        elif kind == "c":
            tk["c"] = last[0] = act([tk["case"]], T.cev[:], P[0][:])
        elif kind == "s":
            t = tt([tk["q"]], T.tf[:], P[2][:, 0:32], T.dump[:], ALU.max)
            last[2] = t = cp([t], T.tu[:], T.tf[:])
            tk["s"] = cp([t, tk["c"], tk["pad"]], T.S[:, 0:VO].indirect(T.tu[:]), T.cev[:])
            for i, (j, c) in enumerate(shifts):
                tk["pk"] = mm([tk["s"], tk["n2"]], P[3][:, j:192:3], T.pk[:, i], T.S[:, SL + 1 + c:SL + 1 + NA:4],
                              i % 2 == 0, i % 2 == 1, mark=(i == 5))
        elif kind == "S":
            if SG_ON_G:
                t = put([tk["s"]], T.sb[:], T.S[:, SL + 1:SL + 1 + NA], [[0, NA]], 1, 0.0)
            else:
                t = act([tk["s"]], T.sb[:], T.S[:, SL + 1:SL + 1 + NA])
            tk["S"] = extract([t, tk["zk"]], P[4][:, 0:16], T.sb, 0, NA, ZK)
            mm([a_fill], P[5][:, 0:NA], T.m12[0:1, :], T.lo[0:1, 0:NA], True, False, mark=False)
        elif kind == "L":
            tk["L"] = last[3] = cp([tk["pk"]], T.cel[:], P[3][:, 0:192])
        elif kind == "K":
            tk["K"] = ts([tk["S"]], T.kcu[:], P[4][:, 0:16], 0.5, ALU.subtract)
        elif kind == "k":
            tk["tt"] = ts([tk["K"], tk["zk"]] + [tk["tab%d" % j] for j in range(4)], T.tt[:],
                          T.TAB[:].indirect(T.kcu[:]), -1.0, ALU.mult)
        elif kind == "j":
            if q == "A":
                t = act([tk["tt"]], T.tn[:], T.tt[:], BIG, 0.0, RELU)
            else:
                t = ts([tk["tt"]], T.tn[:], T.tt[:], BIG, ALU.mult, 0.0, ALU.max)
            mm([tk["tt"]], P[5][:, 0:NA], T.idb[:], T.tt[:], False, False, mark=False)
            tk["k"] = mm([t], P[5][:, 0:NA], T.idb[:], T.tn[:], False, True)
        elif kind == "y":
            tk["y"] = ts([tk["k"]], T.yl[:], P[5][:, 0:NA], -1.0, ALU.mult, float(PAD), ALU.add)
        elif kind == "x":
            lo, hi = XC[k], XC[k + 1]
            tx[k] = lin(q, [tk["xb"], tk["L"], a_fill] + upto(tw, UC, NV), T.XL[:, 16 * lo:16 * hi],
                        T.X[:].indirect(T.cel[:, lo:hi]))
        elif kind == "E":
            c0, c1 = CC[k], CC[k + 1]
            for bank, z in zip(BANKS[k], (ZV, ZA)):
                tk["E", bank] = extract(upto(tx, XC, c1) + [last.get(bank), tk["n4"]], P[bank][:, 0:c1 - c0], T.XL,
                                        16 * c0, 16 * c1, z)
        elif kind in ("l", "r"):
            c0, c1 = CC[k], CC[k + 1]
            bank = BANKS[k][kind == "r"]
            lst, done = (T.al, tl) if kind == "l" else (T.vl, tr_)
            done[k] = ts([tk["E", bank]], lst[:, c0:c1], P[bank][:, 0:c1 - c0], C(5), ALU.subtract,
                         float(MID if kind == "l" else TOP), ALU.min)
        elif kind == "p":
            lo, hi = AC[k], AC[k + 1]
            tp[k] = lin(q, upto(tl, CC, hi) + [tk["ch"], tk["pad"]], T.CA[:, 16 * lo:16 * hi],
                        T.CH[:, 0:FO].indirect(T.al[:, lo:hi]))
        elif kind == "q":
            lo, hi = VCUT[k], VCUT[k + 1]
            tq[k] = tt(upto(tr_, CC, hi) + upto(tp, AC, hi) + [arrC], T.S[:, VO + PAD + 16 * lo:VO + PAD + 16 * hi],
                       T.CH[:].indirect(T.vl[:, lo:hi]), T.CA[:, 16 * lo:16 * hi], ALU.add)
        else:
            m0, m1 = YC[k], YC[k + 1]
            n = min(c for c in VCUT if 16 * c >= 12 * m1)
            o = T.Y[:, 16 * m0:16 * m1]
            t = lin(q, upto(tq, VCUT, n) + [tk["y"], a_fill], o,
                    T.S[:, VO:VO + PAD + 16 * n].indirect(T.yl[:, m0:m1]))
            dma("S", [t], [(T.y[:, 16 * m0:16 * m1], o)])

    wait("G", [(s, n) for s, n in cnt.items()])
